import numpy as np, ml_dtypes
CORES = [113,118,241,246]
N = 4
BF = ml_dtypes.bfloat16
W, C, RO, SH = 4096, 384, 5, 4
def parts(rng):
    cov = np.where(rng.random((N, 8, 1, W)) < 0.15, 0, rng.integers(0, 256, (N, 8, 16, W)))
    share = rng.choice(np.array([0.0, 0.1, 0.2, 0.3, 0.5, 0.8]), (N, 8, 1, C))
    tst = np.where(rng.random((N, 8, 16, C)) < share, 256, rng.integers(0, 256, (N, 8, 16, C)))
    return cov, tst, rng.integers(0, 160, (N, 8, 16, C)), rng.integers(200, 2000, (N, 8))
def pack(cov, tst, pr, th):
    return {"cov": np.ascontiguousarray(cov.reshape(N, 128, W)).astype(np.float32).astype(BF), "tst": np.ascontiguousarray(tst.reshape(N, 128, C)).astype(np.int32),
            "pr": np.ascontiguousarray(pr.reshape(N, 128, C)).astype(np.float32).astype(BF), "th": np.ascontiguousarray(th.reshape(N, 8, 1)).astype(np.int32)}
def setup_inputs(rng):
    return pack(*parts(rng))
def setup_inputs_corners(rng):
    cov, tst, pr, th = parts(rng)
    c = np.arange(C); lane = np.arange(16)[:, None]; full = rng.integers(0, 256, (N, 8, 16, C))
    th = rng.choice(np.array([0, 1, 500, 4080]), (N, 8))
    for r in range(N):
        for g in range(8):
            k = (g + r) % 8; x = full[r, g]
            if k == 1: x = np.full((16, C), 256)
            elif k == 2: x = np.where(lane == c % 16, 256, x)
            elif k == 3: x = np.where((lane + c) % 2 == 1, 256, x)
            elif k == 4:
                x = np.repeat(x[:, :1], C, axis=1); pr[r, g] = np.repeat(pr[r, g][:, :1], C, axis=1); th[r, g] = 0
            elif k == 5: x = np.where((lane == c % 16) | (lane == (c + 1) % 16), x, 256)
            elif k == 6:
                cov[r, g][:, rng.random(W) < 0.7] = 0; th[r, g] = 0
            elif k == 7: pr[r, g] = 255 * rng.integers(0, 2, (1, C))
            tst[r, g] = x
    q = rng.permutation(N); th[q[0]] = 0; th[q[1]] = 4080
    r = int(q[0]); g = (8 - r) % 8
    cov[r, g, 0] = 0; cov[r, g, 1:] = rng.integers(1, 256, (15, W))
    pr[r, g, :, 0::2] = 255; pr[r, g, :, 1::2] = 0
    k = np.arange(C // 2); p = 1 + k % 14; v = rng.integers(0, 256, (2, C // 2)); x = np.full((16, C), 256)
    for odd in range(2):
        x[p, 2 * k + odd] = v[0]; x[p + 1, 2 * k + odd] = v[1]
    tst[r, g] = x
    return pack(cov, tst, pr, th)
def pairs(rng, low):
    x = rng.integers(0, 256, 2 ** 15); y = rng.integers(0, 256, 2 ** 15); i = rng.integers(0, 16, 2 ** 15)
    col, at = np.unique(((((2 * x + 1) * (2 * y + 1)) >> 4) + 613 * i) & (W - 1), return_index=True)
    at = rng.permutation(at[col >= low])
    return x[at], y[at], i[at]
def lone(rng, x, y, i):
    k = len(x); c = np.arange(k); v = np.full((16, k), 256)
    v[i, c] = x; v[(i + 1) & 15, c] = y
    for d in range(3, 15, 2): v[(i + d) & 15, c] = rng.integers(0, 256, k)
    return v
def setup_inputs_crowd(rng):
    cov, tst, pr, th = parts(rng)
    a = int(rng.integers(0, N)); b = (a + 1) % N; d = (a + 2) % N
    v = rng.integers(0, 256, (8, 16, C)); v[:, [1, 5, 7, 9, 11, 13, 15]] = 256
    tst[a] = v; th[a] = rng.integers(511, 1500, 8); th[b] = 0; th[d] = 0
    cov[b] = rng.integers(1, 256, (8, 16, W)); cov[d] = rng.integers(1, 256, (8, 16, W))
    c = np.arange(C); second = ((c % 2 == 0) & (c > 0)) | (c == C - 1)
    for g in range(8):
        p = np.append(rng.permutation(C - 1)[:31], C - 1)
        few = ((((2 * v[g, 2, p] + 1) * (2 * v[g, 3, p] + 1)) >> 4) + 613 * 2) & (W - 1)
        most = ((((2 * v[g, 3, p] + 1) * (2 * v[g, 4, p] + 1)) >> 4) + 613 * 3) & (W - 1)
        cov[a, g][:, few] = 255; cov[a, g][int(rng.integers(0, 16)), few] = 254; cov[a, g][:, most] = 255
        x, y, i = pairs(rng, 0)
        tst[b, g] = lone(rng, x[:C], y[:C], i[:C])
        x, y, i = pairs(rng, W - 254 if g == 7 else 0)
        o = (c + 1) // 2; o[C - 1] = 0; o = np.where(o > 0, 1 + (o - 1) % (len(x) - 1), 0)
        tst[d, g] = lone(rng, x[o], y[o], i[o])
        lev = rng.integers(0, 16, C // 2)[o]; lev = np.where(second, (lev + rng.integers(1, 16, C)) & 15, lev)
        pr[d, g] = np.where(np.arange(16)[:, None] == lev[None, :], 0, 255)
    return pack(cov, tst, pr, th)
def setup_inputs_ties(rng):
    unit = np.where(np.arange(8) % 4 == 1, 1, 85).reshape(1, 8, 1, 1)
    cov = unit * np.where(rng.random((N, 8, 1, W)) < 0.5, rng.integers(0, 4, (N, 8, 1, W)), rng.integers(0, 4, (N, 8, 16, W)))
    pr = unit * np.where(rng.random((N, 8, 1, C)) < 0.5, rng.integers(0, 2, (N, 8, 1, C)), rng.integers(0, 2, (N, 8, 16, C)))
    few = rng.choice(np.array([0, 1, 64, 128, 255, 256]), (N, 8, 16, C)); many = np.where(rng.random((N, 8, 16, C)) < 0.2, 256, rng.integers(0, 256, (N, 8, 16, C)))
    tst = np.where(rng.random((N, 8, 1, C)) < 0.5, few, many)
    return pack(cov, tst, pr, unit[..., 0, 0] * rng.integers(0, 24, (N, 8)))
def setup_inputs_spread(rng):
    cov = np.minimum((np.exp2(8 * rng.random((N, 8, 1, W))) * rng.random((N, 8, 16, W)) * 1.01).astype(np.int64), 255)
    pr = np.minimum((np.exp2(8 * rng.random((N, 8, 16, C))) * rng.random((N, 8, 1, C))).astype(np.int64), 255)
    tst = np.minimum((256 * rng.random((N, 8, 16, C)) ** rng.choice(np.array([0.25, 1.0, 4.0]), (N, 8, 16, 1))).astype(np.int64), 255)
    tst = np.where(rng.random((N, 8, 16, C)) < rng.random((N, 8, 1, C)) * 0.6, 256, tst)
    th = np.minimum(np.exp2(12 * rng.random((N, 8))).astype(np.int64) - 1, 4080)
    return pack(cov, tst, pr, th)
def setup_inputs_ends(rng):
    kind = rng.integers(0, 3, (N, 8, 1, W)); cov = 255 * np.where(kind == 2, rng.integers(0, 2, (N, 8, 16, W)), kind)
    lane = np.arange(16)
    for t in range(RO):
        z = (613 * lane + 77 * t) & (W - 1); f = ((511 * 511 >> 4) + 613 * lane + 77 * t) & (W - 1)
        cov[..., z] = 255; cov[..., f] = 0; cov[..., f[15]] = 255; cov[:, ::2, :, f[6]] = 255
    u = rng.random((N, 8, 16, C))
    tst = np.where(u < 0.5, 0, np.where(u < 0.7, 256, np.where(u < 0.9, 255, rng.integers(0, 256, (N, 8, 16, C)))))
    tst[..., [2, C - 1]] = 0; tst[..., [5, C - 2]] = 255; tst[..., [1, C - 3]] = 256
    pr = 255 * rng.integers(0, 2, (N, 8, 16, C))
    pr[..., [2, 5, C - 2, C - 1]] = 255; pr[:, :, 15, [2, 5, C - 2, C - 1]] = 0; pr[:, 1::2, 4, [2, C - 1]] = 0
    o = np.argsort(rng.random((N, 8)), axis=1); th = 4080 * (o < rng.integers(3, 6, (N, 1))).astype(np.int64)
    th[N - 1, 7] = 4080; th[N - 1, 0] = 0
    return pack(cov, tst, pr, th)
def check_inputs(d):
    bad = []
    for k, lo, hi in (("cov", 0, 255), ("tst", 0, 256), ("pr", 0, 255), ("th", 0, 4080)):
        v = np.asarray(d[k]).astype(np.float64)
        if not (np.min(v) >= lo and np.max(v) <= hi): bad.append("range of " + k)
        elif np.any(v != np.floor(v)): bad.append("whole numbers in " + k)
    return bad
def reference(cov, tst, pr, th):
    U = cov.astype(np.float32).astype(np.int64).reshape(N, 8, 16, W); T = tst.astype(np.int64).reshape(N, 8, 16, C)
    price = pr.astype(np.float32).astype(np.int64).reshape(N, 8, 16, C); lim = th.astype(np.int64).reshape(N, 8, 1)
    lane = np.arange(16).reshape(1, 16, 1); last = np.zeros(N, np.int64)
    for t in range(RO):
        rho = (5 * t) & 15; now = np.zeros(N, np.int64)
        for r in range(N):
            s = (r + t) % N
            x = T[r]; y = np.roll(x, -(1 + t), axis=1)
            live = (x != 256) & (y != 256)
            code = ((((2 * x + 1) * (2 * y + 1)) >> 4) + 613 * lane + 77 * t) & (W - 1)
            got = np.take_along_axis(U[s], code.reshape(8, 1, 16 * C), 2).reshape(8, 16, 16, C)
            gain = np.add.reduce(np.where(live[:, None], np.maximum(got - price[s][:, :, None, :], 0), 0), axis=2)
            lev = np.argmax(gain, axis=1); best = np.max(gain, axis=1)
            useful = best >= lim[s] + (last[s] & 255); now[s] = np.sum(~useful)
            some = np.any(live, axis=1)
            vote = np.argmax(np.where(live, np.add.reduce(got, axis=1), -1), axis=1)
            taken = np.take_along_axis(code, vote[:, None, :], 1)[:, 0] >> SH
            most = np.argmax(np.where(live, np.take_along_axis(got, lev[:, None, None, :], 1)[:, 0], -1), axis=1)
            credit = np.take_along_axis(code, most[:, None, :], 1)[:, 0]
            none = x == 256; first = np.argmax(none, axis=1)
            new = np.array(x)
            g, c = np.nonzero(~useful & some & np.any(none, axis=1))
            new[g, first[g, c], c] = taken[g, c]
            new[:, rho] = np.where(useful, 16 * lev + (best & 15), 256)
            for g in range(8):
                c = np.nonzero(useful[g] & some[g])[0]
                col, at = np.unique(credit[g, c], return_index=True)
                U[s, g, lev[g, c[at]], col] = 0
            T[r] = new
        last = now
    left = np.add.reduce(U.reshape(N, 128, W // 16, 16), axis=3)
    return {"yt": T.reshape(N, 128, C).astype(np.float32), "yc": left.astype(np.float32)}

@@ -1,0 +1,529 @@
+import numpy as np
+from concourse.mybir import AluOpType as ALU, AxisListType as AX, ActivationFunctionType as AF
+
+C, W, RO = 384, 4096, 5
+VOID = -128.0
+UW = W + 32
+GTW = 16 * C + 16
+MAGIC = 8388608.0
+BIG = 1.0e9
+
+SCRATCH = {}
+SEMAPHORES = ["sv", "sa", "sp", "sg", "ld0", "ld1", "ld2", "ld3", "ld4", "st0", "st1", "out", "out2"] + ["arr%d" % t for t in range(RO)]
+VIEW = {}
+
+
+def _pack(buf, names, cols, dtype):
+    step = -(-cols // 32) * 32
+    for k, n in enumerate(names.split()):
+        VIEW[n] = (buf, k * step, cols)
+    SCRATCH[buf] = ("sbuf", [128, step * len(names.split())], dtype)
+
+
+def _sb(names, cols, dtype):
+    for n in names.split():
+        SCRATCH[n] = ("sbuf", [128, cols], dtype)
+
+
+_sb("U", UW, "bfloat16")
+_sb("tsti pi3 t2 t3 KS VS MS", C, "int32")
+_sb("prb prp nn hib FO FQ E2 E2T ones MO nBQ nB Eq lost RSb V wt x0 x1 x2 x3 x4 xo0 xo1", C, "bfloat16")
+_sb("aS t1 h0 h1 KQ KVQ KM MD RBs yo RS", C, "float32"), _sb("cf xd", C, "float16")
+_sb("got R", 16 * C, "bfloat16")
+_sb("GT", GTW, "bfloat16")
+_sb("yco", 256, "float32")
+_sb("RY", W // 2, "bfloat16"), _sb("ys", W // 2, "float32")
+_sb("cu", C, "uint16")
+_sb("rep rep15 wl oG", 32, "uint16"), _sb("oS", 48, "uint16")
+_pack("packI", "K Ai Bi Av xp thi mi ma", 24, "int32")
+_pack("packF", "z z8 Cc Dd us Ee al lz tkm xpf thr thb thR zr mf thf", 24, "float32")
+_pack("packB", "val tkb CWh CWl", 24, "bfloat16")
+_sb("pc", 32, "int32"), _sb("pf", 32, "float32")
+_sb("uA mB sL sG sH", 128, "int32"), _sb("sT0 sT1", 128, "int32"), _sb("iN", 160, "int32")
+_sb("uM uD", 128, "float32")
+_sb("rK", RO * 128, "int32"), _sb("rKh rKl", RO * 128, "int32"), _sb("rKhb rKlb", RO * 128, "bfloat16")
+_sb("r1", 128, "int32"), _sb("rH rV rM", 128, "bfloat16")
+_sb("I1 Iv I16 I64k Im256 Blk TriM T00 T01 T10 T11 PL8", 128, "bfloat16")
+_pack("packP", " ".join("P2_%d Pn_%d Cm_%d Ir_%d" % (t, t, t, t) for t in range(RO)), 128, "bfloat16")
+_sb("Z", 144, "bfloat16"), _sb("J0 J1", 160, "float16")
+_sb("PLf onf THl", 128, "float32"), _sb("G2f I1h", 128, "float16")
+for _k in range(8):
+    SCRATCH["B%d" % _k] = ("psum", [128, 512], "float32")
+
+CHUNKS = [(0, 64), (64, 192), (192, 320), (320, 384)]
+GATH = [[("a", 0, 32), ("v", 32, 64)], [("a", 64, 192)], [("a", 192, 320)], [("a", 320, 384)]]
+NCH = len(CHUNKS)
+VOTES = [[0], [1], [], [], [2, 3]]
+
+
+def rank_program(g, core, T, topo):
+    rank = T.rank_of(core)
+    if rank is None:
+        return
+    Q = {"v": g.vector, "a": g.scalar, "p": g.tensor, "g": g, "y": g.sync}
+    sem = {"v": T.sem.sv, "a": T.sem.sa, "p": T.sem.sp, "g": T.sem.sg}
+    cnt, clock, snap, hist = {}, {e: {} for e in Q}, {}, {}
+
+    def A(name, c0=0, c1=None, step=1, p=128):
+        name, base, cols = VIEW.get(name, (name, 0, SCRATCH.get(name, (0, (0, 0)))[1][1]))
+        c0, c1 = base + c0, base + (cols if c1 is None else c1)
+        ap = T[name][0:p, c0:c1:step] if step != 1 else T[name][0:p, c0:c1]
+        return (ap, name, c0, c1, step)
+
+    def IND(win, off):
+        return (win[0].indirect(off[0]),) + tuple(win[1:])
+
+    def meet(a, b):
+        if a[1] >= b[2] or b[1] >= a[2]:
+            return False
+        if a[3] == b[3] and a[3] > 1 and (a[1] - b[1]) % a[3]:
+            return False
+        return True
+
+    def need(e, reads, writes):
+        want = {}
+
+        def ask(f, n):
+            want[f] = max(want.get(f, 0), n)
+        for x, wr in [(x, False) for x in reads] + [(x, True) for x in writes]:
+            ps = SCRATCH[x[1]][0] == "psum"
+            for h in hist.get(x[1], []):
+                hit = meet((0,) + tuple(x[2:]), (0,) + h[1:4])
+                if h[4] != e:
+                    if ps or (hit and (wr or h[6])):
+                        ask(h[4], h[5])
+                elif hit and (wr or h[6]) and e != "p":
+                    ask(h[4], h[5])
+        for f in sorted(want, key=lambda k: -want[k]):
+            if clock[e].get(f, 0) < want[f]:
+                Q[e].wait_ge(sem[f], want[f])
+                for k, n in snap[(f, want[f])].items():
+                    clock[e][k] = max(clock[e].get(k, 0), n)
+                clock[e][f] = max(clock[e].get(f, 0), want[f])
+
+    def note(f, n, e, reads, writes):
+        snap[(f, n)] = dict(clock[e])
+        for x in writes:
+            old = hist.get(x[1], [])
+            hist[x[1]] = [h for h in old if not (x[4] == 1 and h[1] >= x[2] and h[2] <= x[3] and (clock[e].get(h[4], 0) >= h[5] or h[4] == f))]
+            hist[x[1]].append((0, x[2], x[3], x[4], f, n, True))
+        for x in reads:
+            L = hist.setdefault(x[1], [])
+            L[:] = [h for h in L if not (not h[6] and h[4] == f and h[1:4] == tuple(x[2:5]))]
+            L.append((0, x[2], x[3], x[4], f, n, False))
+
+    def run(e, make, reads, writes):
+        need(e, reads, writes)
+        ins = make(Q[e])
+        cnt[e] = cnt.get(e, 0) + 1
+        ins.then_inc(sem[e], 1)
+        note(e, cnt[e], e, reads, writes)
+
+    def dma(e, out, in_, s, oap=None, iap=None):
+        reads, writes = [x for x in (in_,) if x], [x for x in (out,) if x]
+        need(e, reads, writes)
+        Q[e].dma_start(out[0] if out else oap, in_[0] if in_ else iap).then_inc(T.sem[s], 16)
+        sem[s] = T.sem[s]
+        cnt[s] = cnt.get(s, 0) + 16
+        note(s, cnt[s], e, reads, writes)
+
+    def mm(out, l, r, start, stop):
+        run("p", lambda q: q.matmul(out[0], l[0], r[0], start, stop), [l, r], [out])
+
+    def tt(out, a, b, op, xr=()):
+        run("v", lambda q: q.tensor_tensor(out[0], a[0], b[0], op), [a, b] + list(xr), [out])
+
+    def ts(out, a, s1, op0, s2=None, op1=None):
+        xr = [s for s in (s1, s2) if isinstance(s, tuple)]
+        v1 = s1[0] if isinstance(s1, tuple) else s1
+        v2 = s2[0] if isinstance(s2, tuple) else s2
+        if op1 is None:
+            run("v", lambda q: q.tensor_scalar(out[0], a[0], v1, None, op0), [a] + xr, [out])
+        else:
+            run("v", lambda q: q.tensor_scalar(out[0], a[0], v1, v2, op0, op1), [a] + xr, [out])
+
+    def cp(out, a, xr=()):
+        run("v", lambda q: q.tensor_copy(out[0], a[0]), [a] + list(xr), [out])
+
+    def turn(out, a):
+        run("v", lambda q: q.transpose(out[0], a[0]), [a], [out])
+
+    def ms(out, c):
+        run("v", lambda q: q.memset(out[0], c), [], [out])
+
+    def act(out, a, func=AF.Copy, xr=(), **kw):
+        run("a", lambda q: q.activation(out[0], a[0], func, **kw), [a] + list(xr), [out])
+
+    def iota(out, pattern, base, cm):
+        run("g", lambda q: q.iota(out[0], pattern, base, cm), [], [out])
+
+    def sel(out, a, pattern, op, fill, base, cm):
+        run("g", lambda q: q.affine_select(out[0], a[0], pattern, op, fill, base, cm), [a], [out])
+
+    B = lambda k, c0=0, c1=C, step=1: A("B%d" % k, c0, c1, step)
+
+    def top(out, src, reset):
+        run("v", lambda q: q.tensor_tensor_scan(out[0], reset[0], src[0], -BIG, ALU.min, ALU.max), [src, reset], [out])
+
+    LAST = lambda n: A(n, 15, C, 16)
+
+    dma("y", A("tsti"), None, "ld0", iap=T.tst[:])
+    dma("a", A("prb"), None, "ld1", iap=T.pr[:])
+    dma("a", A("thi", 0, 1, 1, 8), None, "ld2", iap=T.th[:])
+    dma("y", A("U", 0, 2048), None, "ld3", iap=T.cov[:, 0:2048])
+    dma("a", A("U", 2048, 4096), None, "ld4", iap=T.cov[:, 2048:4096])
+
+    iota(A("pc", 0, 1), [[0, 1]], 0, 1)
+    iota(A("uA"), [[-1, 128]], 256, 1)
+    iota(A("mB"), [[1, 8], [0, 16]], 0, 0)
+    iota(A("rK"), [[77, RO], [0, 8], [613, 16]], 0, 0)
+    iota(A("r1"), [[0, 8], [-1, 16]], 15, 0)
+    iota(A("iN"), [[1, 160]], -16, 0)
+    iota(A("K"), [[1, 24]], 0, 0)
+    iota(A("pi3"), [[0, 24], [1, 16]], 0, 0)
+    iota(A("sL"), [[32, 4], [1, 2], [2, 16]], 0, 0)
+    iota(A("sG"), [[2, 4], [0, 16], [1, 2]], 0, 0)
+    iota(A("sH"), [[1, 4], [0, 32]], 0, 0)
+    ms(A("ones"), 1.0)
+    P = lambda k: A("pc", k, k + 1)
+    F = lambda k: A("pf", k, k + 1)
+    ts(P(1), P(0), 4, ALU.arith_shift_right)
+    ts(P(3), P(0), 15, ALU.bitwise_and)
+    ts(P(2), P(1), 16, ALU.mult)
+    cp(A("pf", 0, 4), A("pc", 0, 4))
+    ts(A("uA"), A("uA"), 15, ALU.bitwise_and)
+    ts(A("uD"), A("mB"), F(1), ALU.subtract, -16.0, ALU.mult)
+    tt(A("uM"), A("uA"), A("uD"), ALU.add)
+    ts(A("Iv"), A("uM"), 0.0, ALU.is_equal, -360448.0, ALU.mult)
+
+    def perms(t):
+        ts(A("P2_%d" % t), A("uM"), t + 1.0, ALU.is_equal, 2.0, ALU.mult)
+        act(A("Pn_%d" % t), A("P2_%d" % t), scale=-256.0)
+        ts(A("Cm_%d" % t), A("uM"), t + 1.0, ALU.is_equal, -131072.0, ALU.mult)
+        tt(A("Cm_%d" % t), A("Cm_%d" % t), A("Iv"), ALU.add)
+
+    def restmats(t):
+        ts(F(12 + t), F(3), float(5 * t % 16), ALU.not_equal)
+        act(A("Ir_%d" % t), A("I1"), scale=F(12 + t)[0], xr=[F(12 + t)])
+    perms(0)
+    row = lambda n, c0=0: A(n, c0, c0 + 128, 1, 1)
+    one = lambda c0=0, c1=C: A("ones", c0, c1, 1, 1)
+
+    def rows(c0, c1):
+        R0 = lambda n: A(n, c0, c1, 1, 1)
+        ts(R0("rKh"), R0("rK"), 8, ALU.arith_shift_right, 15, ALU.bitwise_and)
+        ts(R0("rKhb"), R0("rKh"), 4096.0, ALU.mult)
+        ts(R0("rKl"), R0("rK"), 255, ALU.bitwise_and)
+        ts(R0("rKlb"), R0("rKl"), 16.0, ALU.mult)
+    rows(0, 128)
+    for b in range(2):
+        cp(A("x0", b, C, 2), A("tsti", 192 * b, 192 * b + 192))
+
+    def constants2():
+        ms(A("U", W, W + 16), VOID)
+        ms(A("U", W + 16, UW), 0.0)
+        ts(A("I1"), A("uM"), 0.0, ALU.is_equal)
+        act(A("I16"), A("I1"), scale=16.0)
+        act(A("Im256"), A("I1"), scale=-256.0)
+        act(A("I64k"), A("I1"), scale=65536.0)
+        for b in range(2):
+            act(A("prp", b, C, 2), A("prb", 192 * b, 192 * b + 192))
+        for b in range(2):
+            cp(B(0, b, C, 2), A("prb", 192 * b, 192 * b + 192))
+        cp(row("rH"), row("r1"))
+        ts(row("rV"), row("r1"), 256.0, ALU.mult)
+        ts(row("rM"), row("r1"), 4096.0, ALU.mult, 2048.0, ALU.add)
+
+    def constants3():
+        ts(A("Z"), A("iN", 0, 144), F(2), ALU.is_equal, 4096.0, ALU.mult)
+        ts(P(11), P(1), 1, ALU.bitwise_and)
+        ts(P(8), P(11), 999, ALU.mult)
+        ts(P(9), P(11), 999, ALU.mult, -999, ALU.add)
+        tt(P(8), P(0), P(8), ALU.subtract)
+        tt(P(9), P(0), P(9), ALU.add)
+        ts(P(4), P(0), 1, ALU.bitwise_and)
+        ts(P(5), P(0), 31, ALU.bitwise_and)
+        ts(P(6), P(0), 1, ALU.arith_shift_right)
+        ts(P(7), P(0), 5, ALU.arith_shift_right)
+        ts(P(5), P(5), 1, ALU.arith_shift_right)
+        ts(P(7), P(7), 2, ALU.mult)
+        ts(P(10), P(3), W + 16, ALU.add)
+        tt(P(7), P(7), P(4), ALU.add)
+        cp(A("pf", 4, 12), A("pc", 4, 12))
+        ts(A("I1h"), A("uM"), 0.0, ALU.is_equal)
+        for g2 in range(2):
+            ts(A("J%d" % g2), A("iN"), F(8 + g2), ALU.is_equal)
+        ts(A("Blk"), A("mB"), F(1), ALU.is_equal)
+        sel(A("TriM"), A("Blk"), [[1, 128]], ALU.is_gt, 0.0, 0, -1)
+        ms(A("sT0"), -1000), ms(A("sT1"), -1000)
+        iota(A("sT0", 0, 128, 2), [[32, 4], [1, 2], [2, 8]], 0, 0)
+        iota(A("sT1", 1, 128, 2), [[32, 4], [1, 2], [2, 8]], 0, 0)
+        tt(A("TriM"), A("TriM"), A("I1"), ALU.subtract)
+        ms(A("RS"), BIG)
+        sel(A("RS"), A("RS"), [[0, 24], [1, 16]], ALU.not_equal, -BIG, 0, 0)
+
+    def constants4():
+        ms(A("GT", 16 * C, GTW), VOID)
+        for q3 in range(2):
+            for g2 in range(2):
+                ts(A("T%d%d" % (q3, g2)), A("sT%d" % g2), 16.0 * q3, ALU.add, F(0), ALU.is_equal)
+        ts(A("CWh"), A("K", 0, 24), 256.0, ALU.mult)
+        ts(A("CWl"), A("ones", 0, 24), F(3), ALU.mult, 16.0, ALU.mult)
+        ts(A("CWl"), A("CWl"), 15.0, ALU.add)
+        cp(A("rep", 0, 24), A("K", 0, 24))
+        ts(A("rep15", 0, 24), A("K", 0, 24), 16.0, ALU.mult, 15.0, ALU.add)
+        cp(A("thf", 0, 1, 1, 8), A("thi", 0, 1, 1, 8))
+        ts(A("mi", 0, 24), A("K", 0, 24), 1, ALU.bitwise_and)
+        ts(A("thR", 0, 24, 1, 8), A("mi", 0, 24, 1, 8), A("pf", 4, 5, 1, 8), ALU.is_equal, 16.0, ALU.mult)
+        ts(A("thR", 0, 24, 1, 8), A("thR", 0, 24, 1, 8), A("thf", 0, 1, 1, 8), ALU.mult)
+        ts(A("THl", 0, 128, 1, 8), A("sH", 0, 128, 1, 8), A("pf", 6, 7, 1, 8), ALU.is_equal)
+        mm(B(7, 0, 24), A("THl", 0, 128, 1, 8), A("thR", 0, 24, 1, 8), True, True)
+        restmats(0)
+
+    def constants5():
+        ts(A("MD"), A("pi3"), F(5), ALU.is_equal)
+        ts(A("MO"), A("pi3"), F(5), ALU.is_ge, 32768.0, ALU.mult)
+        ts(A("PLf"), A("sL"), F(0), ALU.is_equal)
+        act(A("PL8"), A("PLf"), scale=8192.0)
+        ts(A("G2f"), A("sG"), F(7), ALU.is_equal)
+        act(A("onf"), A("I1"), AF.Identity, scale=0.0, bias=1.0)
+        act(A("RSb"), A("RS"))
+
+    def constants6(t):
+        rows(128 * t, 128 * t + 128)
+        perms(t)
+        restmats(t)
+
+    def constants7():
+        act(A("RY"), A("got", 0, W // 2), AF.Identity, scale=0.0, bias=1.0)
+        sel(A("RY"), A("RY"), [[0, W // 32], [1, 16]], ALU.not_equal, 0.0, 0, 0)
+
+    def codes1(t):
+        x = A("x%d" % t)
+        mm(B(2), one(0, 128), one(), True, False)
+        mm(B(3), row("rKhb", 128 * t), one(), True, False)
+        mm(B(3), row("rKlb", 128 * t), one(), False, False)
+        act(A("nn"), x, AF.Relu, bias=-255.0)
+        act(A("aS"), x, AF.Identity, bias=1.0, scale=2.0)
+        mm(B(2), A("P2_%d" % t), x, False, False)
+        mm(B(2), A("Pn_%d" % t), A("nn"), False, True)
+        mm(B(3), A("Cm_%d" % t), A("nn"), False, True)
+
+    def codes2(t):
+        for c0, c1 in (CHUNKS[0], (CHUNKS[0][1], C)):
+            tt(A("t1", c0, c1), A("aS", c0, c1), B(2, c0, c1), ALU.mult)
+            tt(A("t2", c0, c1), A("t1", c0, c1), B(3, c0, c1), ALU.add)
+            ts(A("t3", c0, c1), A("t2", c0, c1), 4, ALU.arith_shift_right, 0x8FFF, ALU.bitwise_and)
+            ts(A("cu", c0, c1), A("t3", c0, c1), 4096, ALU.min)
+
+    def starts(t):
+        mm(B(4), row("rH"), one(), True, False)
+        mm(B(4), A("Im256"), A("prp"), False, False)
+        mm(B(5), row("rV"), one(), True, False)
+
+    def starts2(t):
+        mm(B(3), A("TriM"), A("nn"), True, False)
+        mm(B(3), one(0, 128), one(), False, True)
+        mm(B(1), A("I1h"), A("cf"), True, True)
+        mm(B(6), row("rM"), one(), True, False)
+        for b in range(2):
+            for g2 in range(2):
+                s = 16 + 16 * (g2 - b)
+                mm(B(6, g2, C, 2), A("J%d" % g2, s, s + 128), A("cf", b, C, 2), False, False)
+
+    def highs(t):
+        act(A("h0"), B(1), AF.Identity, bias=128.0 - 0.46875, scale=0.0625)
+        act(A("h1"), A("h0"), AF.Identity, bias=MAGIC)
+        act(A("FO"), B(3), AF.Relu, bias=1.0, scale=-1.0)
+        act(A("hib"), A("h1"), AF.Identity, bias=-MAGIC)
+
+    def gather(k):
+        for e, c0, c1 in GATH[k]:
+            out, win, off = A("got", 16 * c0, 16 * c1), A("U"), A("cu", c0, c1)
+            (act if e == "a" else cp)(out, IND(win, off), xr=[off])
+
+    def price(k):
+        c0, c1 = CHUNKS[k]
+        for i in range(16):
+            tt(A("R", C * i + c0, C * i + c1), A("got", 16 * c0 + i, 16 * c1, 16), B(0, c0, c1), ALU.max)
+
+    def gains(k):
+        c0, c1 = CHUNKS[k]
+        for i in range(16):
+            mm(B(4, c0, c1), A("I16"), A("R", C * i + c0, C * i + c1), False, k == NCH - 1 and i == 15)
+
+    def votes(k):
+        c0, c1 = CHUNKS[k]
+        for i in range(16):
+            mm(B(5, c0, c1), A("Z", 16 - i, 144 - i), A("got", 16 * c0 + i, 16 * c1, 16), False, False)
+
+    def gturn(k):
+        c0, c1 = CHUNKS[k]
+        turn(A("GT", 16 * c0, 16 * c1), A("got", 16 * c0, 16 * c1))
+
+    def best1(t):
+        turn(A("KQ"), B(4))
+        top(A("KS"), A("KQ"), A("RS"))
+        ts(A("Ai"), LAST("KS"), 15, ALU.bitwise_and)
+        tt(A("z"), LAST("KS"), A("thr"), ALU.is_lt)
+        ts(A("z8"), A("z"), 8192.0, ALU.mult)
+        tt(A("val"), A("z8"), A("Ai"), ALU.subtract)
+        mm(B(7, 0, 24), A("I1"), A("CWh"), True, False)
+        mm(B(7, 0, 24), A("I1"), A("CWl"), False, False)
+        for q3 in range(2):
+            for g2 in range(2):
+                mm(B(7, q3, 24, 2), A("T%d%d" % (q3, g2)), A("val", g2, 24, 2), False, q3 == 1 and g2 == 1)
+
+    def best2(t):
+        ts(A("wl", 0, 24), B(7, 0, 24), 16.0 * C, ALU.min)
+        act(A("wt"), IND(A("GT"), A("wl", 0, 24)), xr=[A("wl", 0, 24)])
+        mm(B(6), A("I64k"), A("wt"), False, True)
+
+    def notb(t):
+        tt(A("nBQ"), IND(A("KS"), A("rep15", 0, 24)), A("KQ"), ALU.not_equal, xr=[A("rep15", 0, 24)])
+        turn(A("nB"), A("nBQ"))
+
+    def level(t):
+        ts(A("Bi"), LAST("KS"), 4, ALU.arith_shift_right, 15, ALU.bitwise_and)
+        ts(A("Cc"), A("Ai"), -16.0, ALU.mult, -16.0, ALU.add)
+        ts(A("us"), A("z"), -1.0, ALU.mult, 1.0, ALU.add)
+        tt(A("Dd"), A("Bi"), A("Cc"), ALU.add)
+        tt(A("Ee"), A("Dd"), A("us"), ALU.mult)
+
+    def vote(t):
+        turn(A("KVQ"), B(5))
+        top(A("VS"), A("KVQ"), A("RS"))
+
+    def update(t):
+        rho, xo = (5 * t) % 16, "xo%d" % (t % 2)
+        ts(A("Av"), LAST("VS"), 255, ALU.bitwise_and)
+        ts(A("al"), LAST("VS"), 0.0, ALU.is_ge)
+        ts(A("tkm"), A("Av"), -256.0, ALU.add)
+        tt(A("lz"), A("al"), A("z"), ALU.mult)
+        tt(A("tkb"), A("tkm"), A("lz"), ALU.mult)
+        tt(A("E2"), IND(A("tkb"), A("rep", 0, 24)), A("FQ"), ALU.mult, xr=[A("rep", 0, 24)])
+        ts(A("E2", rho, C, 16), A("Ee"), 256.0, ALU.add)
+        turn(A("E2T"), A("E2"))
+        mm(B(5), A("Ir_%d" % t), A("x%d" % t), True, False)
+        mm(B(5), A("I1"), A("E2T"), False, True)
+        act(A(xo), B(5))
+        if t < RO - 1:
+            to = T.cores[(rank + 1) % len(T.cores)]
+            rid, pid = topo.addr(to, core)
+            eng = topo.engines(core, to)[:8]
+            need("g", [A(xo)], [])
+            s, a = "st%d" % (t % 2), "arr%d" % (t + 1)
+            g.remote_dma(T["x%d" % (t + 1)][:, :], A(xo)[0], T.sem[a], T.sem[s], pid, rid, sum(1 << k for k in eng))
+            sem[s] = T.sem[s]
+            cnt[s] = cnt.get(s, 0) + len(eng)
+            note(s, cnt[s], "g", [A(xo)], [])
+            src = T.cores[(rank - 1) % len(T.cores)]
+            sem[a], cnt[a] = T.sem[a], len(topo.engines(src, core)[:8])
+            snap[(a, cnt[a])] = {}
+            hist["x%d" % (t + 1)] = [(0, 0, C, 1, a, cnt[a], True)]
+
+    def useless(t):
+        if t == RO - 1:
+            return
+        run("v", lambda q: q.tensor_reduce(A("zr", 0, 1)[0], A("z")[0], AX.X, ALU.add), [A("z")], [A("zr", 0, 1)])
+        mm(B(7, 0, 1), A("onf"), A("zr", 0, 1), True, True)
+        cp(A("mi", 0, 1), B(7, 0, 1))
+        ts(A("ma", 0, 1), A("mi", 0, 1), 255, ALU.bitwise_and)
+        ts(A("mf", 0, 1), A("ma", 0, 1), 16.0, ALU.mult)
+        ts(A("thr"), A("thb"), A("mf", 0, 1), ALU.add)
+
+    HB = (4, 6)
+
+    def claims1(t):
+        turn(A("KM"), B(6))
+        top(A("MS"), A("KM"), A("RS"))
+        ts(A("xp"), LAST("MS"), (1 << 24) | 4095, ALU.bitwise_and)
+        ts(A("xpf"), A("xp"), -2048.0, ALU.add, 32768.0, ALU.min)
+        for h in range(2):
+            c0, c1, rp = 192 * h, 192 * h + 192, A("rep", 12 * h, 12 * h + 12)
+            mm(B(HB[h], c0, c1), A("I1"), A("MO", c0, c1), True, False)
+            tt(A("xd", c0, c1), IND(A("xpf"), rp), A("MD", c0, c1), ALU.mult, xr=[rp])
+            mm(B(HB[h], c0, c1), A("G2f"), A("xd", c0, c1), False, True)
+            act(A("RBs", c0, c1), B(HB[h], c0, c1))
+
+    def claims2(t):
+        for h in range(2):
+            c0, c1, rp = 192 * h, 192 * h + 192, A("rep", 12 * h, 12 * h + 12)
+            tt(A("Eq", c0, c1), IND(A("xpf"), rp), A("RBs", c0, c1), ALU.is_equal, xr=[rp])
+        top(A("lost"), A("Eq"), A("RSb"))
+        mm(B(7, 0, 24), A("PLf"), A("xpf"), True, False)
+        mm(B(7, 0, 24), A("PL8"), LAST("lost"), False, True)
+
+    def claims3(t):
+        for b in range(2):
+            ts(A("oG", 12 * b, 12 * b + 12), B(7, b, 24, 2), 2048.0, ALU.add, F(10), ALU.min)
+        ts(A("oS", 0, 48, 2), B(7, 0, 24), 2048.0, ALU.add, F(10), ALU.min)
+        for b in range(2):
+            o = A("oG", 12 * b, 12 * b + 12)
+            tt(A("V", 192 * b, 192 * b + 192), IND(A("U"), o), A("nB", b, C, 2), ALU.mult, xr=[o])
+        for b in (1, 0):
+            for k in range(11, -1, -1):
+                o = A("oS", 2 * (2 * k + b), 2 * (2 * k + b) + 1)
+                cp(IND(A("U"), o), A("V", 192 * b + 16 * k, 192 * b + 16 * k + 16), xr=[o])
+
+    codes1(0)
+    constants2()
+    constants3()
+    codes2(0)
+    for t in range(RO):
+        starts(t)
+        gather(0)
+        ts(A("cf"), A("t3"), 4096, ALU.min, -2048.0, ALU.add)
+        for k in range(1, NCH):
+            gather(k)
+        starts2(t)
+        for k in range(NCH):
+            price(k)
+            gturn(k)
+            gains(k)
+            for j in VOTES[k]:
+                votes(j)
+            if t == 0 and k == 0:
+                constants4()
+            if t == 0 and k == 1:
+                cp(A("thb"), B(7, 0, 24))
+                cp(A("thr"), A("thb"))
+        best1(t)
+        level(t)
+        best2(t)
+        for j in VOTES[NCH]:
+            votes(j)
+        if t == 0:
+            constants5()
+        highs(t)
+        mm(B(5), A("I1"), A("hib"), False, True)
+        if t < RO - 1:
+            constants6(t + 1)
+        claims1(t)
+        turn(A("FQ"), A("FO"))
+        vote(t)
+        update(t)
+        notb(t)
+        useless(t)
+        claims2(t)
+        if t < RO - 1:
+            codes1(t + 1)
+        if t == 1:
+            constants7()
+        claims3(t)
+        if t < RO - 1:
+            codes2(t + 1)
+
+    top2 = [A("ys"), A("RY"), A("U", 0, W // 2)]
+    run("v", lambda q: q.tensor_tensor_scan(top2[0][0], top2[1][0], top2[2][0], 0.0, ALU.mult, ALU.add), top2[1:], top2[:1])
+    for k in range(16):
+        mm(B(4, 0, 128), A("I1"), A("U", W // 2 + k, W, 16), k == 0, k == 15)
+    for b in range(2):
+        act(A("yo", 192 * b, 192 * b + 192), A("xo0", b, C, 2))
+    dma("a", None, A("yo"), "out", oap=T.yt[:])
+    act(A("yco", 128, 256), B(4, 0, 128))
+    cp(A("yco", 0, 128), A("ys", 15, W // 2, 16))
+    dma("y", None, A("yco"), "out2", oap=T.yc[:])
+    for s in sem:
+        if cnt.get(s, 0):
+            g.wait_ge(sem[s], cnt[s])

@@ -3,9 +3,9 @@ from concourse.mybir import AluOpType as ALU, AxisListType as AX, ActivationFunc
 
 C, W, RO = 384, 4096, 5
 VOID = -128.0
-UW = W + 32
+UW = W + 48
 GTW = 16 * C + 16
-MAGIC = 8388608.0
+MAGIC = 12582912.0
 BIG = 1.0e9
 
 SCRATCH = {}
@@ -27,33 +27,36 @@ def _sb(names, cols, dtype):
 
 _sb("U", UW, "bfloat16")
 _sb("tsti pi3 t2 t3 KS VS MS", C, "int32")
-_sb("prb prp nn hib FO FQ E2 E2T ones MO nBQ nB Eq lost RSb V wt x0 x1 x2 x3 x4 xo0 xo1", C, "bfloat16")
-_sb("aS t1 h0 h1 KQ KVQ KM MD RBs yo RS", C, "float32"), _sb("cf xd", C, "float16")
+_sb("prb prp nn hib FO FQ E2 E2T ones MO nBQ nB V wt x0 x1 x2 x3 x4 xo0 xo1", C, "bfloat16")
+_sb("Eq lost RSb", C + 192, "bfloat16"), _sb("RBs", C + 192, "float32")
+_sb("aS t1 h0 h1 KQ KM MD yo RS", C, "float32"), _sb("cf xd", C, "float16")
 _sb("got R", 16 * C, "bfloat16")
 _sb("GT", GTW, "bfloat16")
 _sb("yco", 256, "float32")
 _sb("RY", W // 2, "bfloat16"), _sb("ys", W // 2, "float32")
 _sb("cu", C, "uint16")
-_sb("rep rep15 wl oG", 32, "uint16"), _sb("oS", 48, "uint16")
-_pack("packI", "K Ai Bi Av xp thi mi ma", 24, "int32")
-_pack("packF", "z z8 Cc Dd us Ee al lz tkm xpf thr thb thR zr mf thf", 24, "float32")
-_pack("packB", "val tkb CWh CWl", 24, "bfloat16")
+_sb("rep rep15 wl oG RP", 32, "uint16")
+_pack("packI", "K Ai Bi Av xp thi mi L1 L2 L3", 24, "int32")
+_pack("packF", "z z8 Cc Dd al lz tkm xpf thr thb thR zr zc ma mb mc mf thf", 24, "float32")
+_pack("packB", "val tkb tkr CWh CWl", 24, "bfloat16")
 _sb("pc", 32, "int32"), _sb("pf", 32, "float32")
 _sb("uA mB sL sG sH", 128, "int32"), _sb("sT0 sT1", 128, "int32"), _sb("iN", 160, "int32")
 _sb("uM uD", 128, "float32")
 _sb("rK", RO * 128, "int32"), _sb("rKh rKl", RO * 128, "int32"), _sb("rKhb rKlb", RO * 128, "bfloat16")
-_sb("r1", 128, "int32"), _sb("rH rV rM", 128, "bfloat16")
+_sb("r1", 128, "int32"), _sb("rH rM", 128, "bfloat16"), _sb("rV", C, "bfloat16")
 _sb("I1 Iv I16 I64k Im256 Blk TriM T00 T01 T10 T11 PL8", 128, "bfloat16")
 _pack("packP", " ".join("P2_%d Pn_%d Cm_%d Ir_%d" % (t, t, t, t) for t in range(RO)), 128, "bfloat16")
-_sb("Z", 144, "bfloat16"), _sb("J0 J1", 160, "float16")
+_sb("BO", 8, "bfloat16"), _sb("HW", 224, "bfloat16"), _sb("X MK", 96, "bfloat16"), _sb("mk", 96, "int32"), _sb("L96", 8, "uint16")
+_sb("J0 J1", 160, "float16")
 _sb("PLf onf THl", 128, "float32"), _sb("G2f I1h", 128, "float16")
 for _k in range(8):
     SCRATCH["B%d" % _k] = ("psum", [128, 512], "float32")
+PB = (0, 1, 7)
 
-CHUNKS = [(0, 64), (64, 192), (192, 320), (320, 384)]
-GATH = [[("a", 0, 32), ("v", 32, 64)], [("a", 64, 192)], [("a", 192, 320)], [("a", 320, 384)]]
+CHUNKS = [(0, 128), (128, 256), (256, 384)]
+GATH = [[("a", 0, 64), ("v", 64, 128)], [("a", 128, 256)], [("a", 256, 384)]]
 NCH = len(CHUNKS)
-VOTES = [[0], [1], [], [], [2, 3]]
+SUMS = [[("v", 0, 128), ("g", 0, 128)], [("v", 128, 256), ("g", 128, 256)], [("g", 256, 384), ("v", 256, 384)], []]
 
 
 def rank_program(g, core, T, topo):
@@ -185,6 +188,7 @@ def rank_program(g, core, T, topo):
     iota(A("sG"), [[2, 4], [0, 16], [1, 2]], 0, 0)
     iota(A("sH"), [[1, 4], [0, 32]], 0, 0)
     ms(A("ones"), 1.0)
+    iota(A("mk"), [[0, 12], [1, 4], [0, 2]], 0, 0)
     P = lambda k: A("pc", k, k + 1)
     F = lambda k: A("pf", k, k + 1)
     ts(P(1), P(0), 4, ALU.arith_shift_right)
@@ -228,14 +232,15 @@ def rank_program(g, core, T, topo):
         act(A("I64k"), A("I1"), scale=65536.0)
         for b in range(2):
             act(A("prp", b, C, 2), A("prb", 192 * b, 192 * b + 192))
-        for b in range(2):
-            cp(B(0, b, C, 2), A("prb", 192 * b, 192 * b + 192))
+        for k in range(3):
+            for j in range(4):
+                mm(B(PB[k], j, 512, 4), A("I1"), A("prp", 128 * k, 128 * k + 128), True, True)
         cp(row("rH"), row("r1"))
-        ts(row("rV"), row("r1"), 256.0, ALU.mult)
+        ts(A("rV", 0, C, 1, 1), A("pi3", 0, C, 1, 1), -256.0, ALU.mult, 3840.0, ALU.add)
         ts(row("rM"), row("r1"), 4096.0, ALU.mult, 2048.0, ALU.add)
 
     def constants3():
-        ts(A("Z"), A("iN", 0, 144), F(2), ALU.is_equal, 4096.0, ALU.mult)
+        ts(A("BO"), A("iN", 16, 24), F(1), ALU.is_equal, 4096.0, ALU.mult)
         ts(P(11), P(1), 1, ALU.bitwise_and)
         ts(P(8), P(11), 999, ALU.mult)
         ts(P(9), P(11), 999, ALU.mult, -999, ALU.add)
@@ -245,11 +250,19 @@ def rank_program(g, core, T, topo):
         ts(P(5), P(0), 31, ALU.bitwise_and)
         ts(P(6), P(0), 1, ALU.arith_shift_right)
         ts(P(7), P(0), 5, ALU.arith_shift_right)
+        ts(P(17), P(0), 5, ALU.arith_shift_right)
+        ts(P(18), P(0), 31, ALU.bitwise_and)
         ts(P(5), P(5), 1, ALU.arith_shift_right)
         ts(P(7), P(7), 2, ALU.mult)
         ts(P(10), P(3), W + 16, ALU.add)
         tt(P(7), P(7), P(4), ALU.add)
         cp(A("pf", 4, 12), A("pc", 4, 12))
+        cp(A("thf", 0, 1, 1, 8), A("thi", 0, 1, 1, 8))
+        ts(A("mi", 0, 24), A("K", 0, 24), 1, ALU.bitwise_and)
+        ts(A("THl", 0, 128, 1, 8), A("sH", 0, 128, 1, 8), A("pf", 6, 7, 1, 8), ALU.is_equal)
+        ts(A("thR", 0, 24, 1, 8), A("mi", 0, 24, 1, 8), A("pf", 4, 5, 1, 8), ALU.is_equal, 16.0, ALU.mult)
+        ts(A("thR", 0, 24, 1, 8), A("thR", 0, 24, 1, 8), A("thf", 0, 1, 1, 8), ALU.mult)
+        mm(B(6, 0, 24), A("THl", 0, 128, 1, 8), A("thR", 0, 24, 1, 8), True, True)
         ts(A("I1h"), A("uM"), 0.0, ALU.is_equal)
         for g2 in range(2):
             ts(A("J%d" % g2), A("iN"), F(8 + g2), ALU.is_equal)
@@ -259,6 +272,8 @@ def rank_program(g, core, T, topo):
         iota(A("sT0", 0, 128, 2), [[32, 4], [1, 2], [2, 8]], 0, 0)
         iota(A("sT1", 1, 128, 2), [[32, 4], [1, 2], [2, 8]], 0, 0)
         tt(A("TriM"), A("TriM"), A("I1"), ALU.subtract)
+        cp(A("thb"), B(6, 0, 24))
+        cp(A("thr"), A("thb"))
         ms(A("RS"), BIG)
         sel(A("RS"), A("RS"), [[0, 24], [1, 16]], ALU.not_equal, -BIG, 0, 0)
 
@@ -272,13 +287,24 @@ def rank_program(g, core, T, topo):
         ts(A("CWl"), A("CWl"), 15.0, ALU.add)
         cp(A("rep", 0, 24), A("K", 0, 24))
         ts(A("rep15", 0, 24), A("K", 0, 24), 16.0, ALU.mult, 15.0, ALU.add)
-        cp(A("thf", 0, 1, 1, 8), A("thi", 0, 1, 1, 8))
-        ts(A("mi", 0, 24), A("K", 0, 24), 1, ALU.bitwise_and)
-        ts(A("thR", 0, 24, 1, 8), A("mi", 0, 24, 1, 8), A("pf", 4, 5, 1, 8), ALU.is_equal, 16.0, ALU.mult)
-        ts(A("thR", 0, 24, 1, 8), A("thR", 0, 24, 1, 8), A("thf", 0, 1, 1, 8), ALU.mult)
-        ts(A("THl", 0, 128, 1, 8), A("sH", 0, 128, 1, 8), A("pf", 6, 7, 1, 8), ALU.is_equal)
-        mm(B(7, 0, 24), A("THl", 0, 128, 1, 8), A("thR", 0, 24, 1, 8), True, True)
         restmats(0)
+
+    def constants4b():
+        cp(A("pf", 17, 19), A("pc", 17, 19))
+        ms(A("HW"), 0.0)
+        ts(A("L1", 0, 6), A("K", 0, 6), 16.0, ALU.mult, F(3), ALU.add)
+        ts(A("L2", 0, 6), A("L1", 0, 6), 43.0, ALU.mult)
+        ts(A("MK"), A("mk"), F(17), ALU.is_equal)
+        ts(A("HW", 96, 128), A("iN", 16, 48), F(18), ALU.is_equal)
+        ts(A("L2", 0, 6), A("L2", 0, 6), 10, ALU.arith_shift_right)
+        ts(A("L3", 0, 6), A("L2", 0, 6), -24.0, ALU.mult)
+        tt(A("L1", 0, 6), A("L1", 0, 6), A("L3", 0, 6), ALU.add)
+        ts(A("L2", 0, 6), A("L2", 0, 6), 2.0, ALU.mult)
+        ts(A("L3", 0, 6), A("L1", 0, 6), 1, ALU.bitwise_and)
+        ts(A("L1", 0, 6), A("L1", 0, 6), 24, ALU.bitwise_and)
+        tt(A("L2", 0, 6), A("L2", 0, 6), A("L3", 0, 6), ALU.add)
+        tt(A("L1", 0, 6), A("L1", 0, 6), A("L2", 0, 6), ALU.add)
+        cp(A("L96", 0, 6), A("L1", 0, 6))
 
     def constants5():
         ts(A("MD"), A("pi3"), F(5), ALU.is_equal)
@@ -286,8 +312,20 @@ def rank_program(g, core, T, topo):
         ts(A("PLf"), A("sL"), F(0), ALU.is_equal)
         act(A("PL8"), A("PLf"), scale=8192.0)
         ts(A("G2f"), A("sG"), F(7), ALU.is_equal)
-        act(A("onf"), A("I1"), AF.Identity, scale=0.0, bias=1.0)
-        act(A("RSb"), A("RS"))
+        act(A("onf"), A("I1"), AF.Identity, scale=0.0, bias=16.0)
+        act(A("RSb", 0, C), A("RS"))
+        act(A("RSb", C, C + 192), A("RS", 0, 192))
+        L1, L2, L3 = A("L1"), A("L2"), A("L3")
+        ts(L1, A("K"), 12.0, ALU.is_ge)
+        ts(L2, L1, -12.0, ALU.mult)
+        tt(L2, L2, A("K"), ALU.add)
+        ts(L1, L1, 2.0, ALU.mult)
+        ts(L3, L2, 1, ALU.bitwise_and)
+        ts(L2, L2, 2.0, ALU.mult)
+        tt(L1, L1, L3, ALU.subtract)
+        tt(L1, L1, L2, ALU.add)
+        cp(A("RP", 0, 24), L1)
+        ts(F(19), F(10), 16.0, ALU.add)
 
     def constants6(t):
         rows(128 * t, 128 * t + 128)
@@ -295,14 +333,16 @@ def rank_program(g, core, T, topo):
         restmats(t)
 
     def constants7():
-        act(A("RY"), A("got", 0, W // 2), AF.Identity, scale=0.0, bias=1.0)
+        act(A("RY"), A("U", 0, W // 2), AF.Identity, scale=0.0, bias=1.0)
         sel(A("RY"), A("RY"), [[0, W // 32], [1, 16]], ALU.not_equal, 0.0, 0, 0)
 
-    def codes1(t):
-        x = A("x%d" % t)
+    def codes0(t):
         mm(B(2), one(0, 128), one(), True, False)
         mm(B(3), row("rKhb", 128 * t), one(), True, False)
         mm(B(3), row("rKlb", 128 * t), one(), False, False)
+
+    def codes1(t):
+        x = A("x%d" % t)
         act(A("nn"), x, AF.Relu, bias=-255.0)
         act(A("aS"), x, AF.Identity, bias=1.0, scale=2.0)
         mm(B(2), A("P2_%d" % t), x, False, False)
@@ -319,12 +359,16 @@ def rank_program(g, core, T, topo):
     def starts(t):
         mm(B(4), row("rH"), one(), True, False)
         mm(B(4), A("Im256"), A("prp"), False, False)
-        mm(B(5), row("rV"), one(), True, False)
+
+    def starts1(t):
+        mm(B(5), one(0, 128), A("rV", 0, C, 1, 1), True, False)
 
     def starts2(t):
         mm(B(3), A("TriM"), A("nn"), True, False)
         mm(B(3), one(0, 128), one(), False, True)
-        mm(B(1), A("I1h"), A("cf"), True, True)
+        mm(B(2), A("I1h"), A("cf"), True, True)
+
+    def starts3(t):
         mm(B(6), row("rM"), one(), True, False)
         for b in range(2):
             for g2 in range(2):
@@ -332,7 +376,7 @@ def rank_program(g, core, T, topo):
                 mm(B(6, g2, C, 2), A("J%d" % g2, s, s + 128), A("cf", b, C, 2), False, False)
 
     def highs(t):
-        act(A("h0"), B(1), AF.Identity, bias=128.0 - 0.46875, scale=0.0625)
+        act(A("h0"), B(2), AF.Identity, bias=128.0 - 0.46875, scale=0.0625)
         act(A("h1"), A("h0"), AF.Identity, bias=MAGIC)
         act(A("FO"), B(3), AF.Relu, bias=1.0, scale=-1.0)
         act(A("hib"), A("h1"), AF.Identity, bias=-MAGIC)
@@ -344,18 +388,23 @@ def rank_program(g, core, T, topo):
 
     def price(k):
         c0, c1 = CHUNKS[k]
-        for i in range(16):
-            tt(A("R", C * i + c0, C * i + c1), A("got", 16 * c0 + i, 16 * c1, 16), B(0, c0, c1), ALU.max)
+        n, f = 4 * (c1 - c0), 4 * (c0 % 128)
+        for s in range(4):
+            r = 4 * C * s + 4 * c0
+            tt(A("R", r, r + n), A("got", 16 * c0 + s, 16 * c1, 4), B(PB[c0 // 128], f, f + n), ALU.max)
 
-    def gains(k):
-        c0, c1 = CHUNKS[k]
+    def gains(c0, c1):
         for i in range(16):
-            mm(B(4, c0, c1), A("I16"), A("R", C * i + c0, C * i + c1), False, k == NCH - 1 and i == 15)
+            r = 4 * C * (i % 4) + i // 4
+            mm(B(4, c0, c1), A("I16"), A("R", r + 4 * c0, r - i // 4 + 4 * c1, 4), False, c1 == C and i == 15)
 
-    def votes(k):
-        c0, c1 = CHUNKS[k]
+    def votes(c0, c1):
         for i in range(16):
-            mm(B(5, c0, c1), A("Z", 16 - i, 144 - i), A("got", 16 * c0 + i, 16 * c1, 16), False, False)
+            mm(B(5, c0 + i, c1, 16), A("got", 16 * c0 + i, 16 * c1, 16), A("BO"), False, False)
+
+    def sums(L):
+        for what, c0, c1 in L:
+            (gains if what == "g" else votes)(c0, c1)
 
     def gturn(k):
         c0, c1 = CHUNKS[k]
@@ -368,16 +417,15 @@ def rank_program(g, core, T, topo):
         tt(A("z"), LAST("KS"), A("thr"), ALU.is_lt)
         ts(A("z8"), A("z"), 8192.0, ALU.mult)
         tt(A("val"), A("z8"), A("Ai"), ALU.subtract)
-        mm(B(7, 0, 24), A("I1"), A("CWh"), True, False)
-        mm(B(7, 0, 24), A("I1"), A("CWl"), False, False)
+        mm(B(4, 0, 24), A("I1"), A("CWh"), True, False)
+        mm(B(4, 0, 24), A("I1"), A("CWl"), False, False)
         for q3 in range(2):
             for g2 in range(2):
-                mm(B(7, q3, 24, 2), A("T%d%d" % (q3, g2)), A("val", g2, 24, 2), False, q3 == 1 and g2 == 1)
+                mm(B(4, q3, 24, 2), A("T%d%d" % (q3, g2)), A("val", g2, 24, 2), False, q3 == 1 and g2 == 1)
 
     def best2(t):
-        ts(A("wl", 0, 24), B(7, 0, 24), 16.0 * C, ALU.min)
+        ts(A("wl", 0, 24), B(4, 0, 24), 16.0 * C, ALU.min)
         act(A("wt"), IND(A("GT"), A("wl", 0, 24)), xr=[A("wl", 0, 24)])
-        mm(B(6), A("I64k"), A("wt"), False, True)
 
     def notb(t):
         tt(A("nBQ"), IND(A("KS"), A("rep15", 0, 24)), A("KQ"), ALU.not_equal, xr=[A("rep15", 0, 24)])
@@ -385,24 +433,27 @@ def rank_program(g, core, T, topo):
 
     def level(t):
         ts(A("Bi"), LAST("KS"), 4, ALU.arith_shift_right, 15, ALU.bitwise_and)
-        ts(A("Cc"), A("Ai"), -16.0, ALU.mult, -16.0, ALU.add)
-        ts(A("us"), A("z"), -1.0, ALU.mult, 1.0, ALU.add)
+        ts(A("Cc"), A("val"), 16.0, ALU.mult, 240.0, ALU.add)
         tt(A("Dd"), A("Bi"), A("Cc"), ALU.add)
-        tt(A("Ee"), A("Dd"), A("us"), ALU.mult)
 
     def vote(t):
-        turn(A("KVQ"), B(5))
-        top(A("VS"), A("KVQ"), A("RS"))
+        top(A("VS"), B(5), A("RS"))
 
     def update(t):
         rho, xo = (5 * t) % 16, "xo%d" % (t % 2)
         ts(A("Av"), LAST("VS"), 255, ALU.bitwise_and)
         ts(A("al"), LAST("VS"), 0.0, ALU.is_ge)
         ts(A("tkm"), A("Av"), -256.0, ALU.add)
-        tt(A("lz"), A("al"), A("z"), ALU.mult)
-        tt(A("tkb"), A("tkm"), A("lz"), ALU.mult)
+        tt(A("tkr"), A("tkm"), A("al"), ALU.mult)
+        tt(A("X"), IND(A("tkr"), A("L96", 0, 6)), A("MK"), ALU.mult, xr=[A("L96", 0, 6)])
+        level(t)
+        for a in range(4):
+            mm(B(5, 0, 24), A("HW", 96 - 32 * a, 224 - 32 * a), A("X", 24 * a, 24 * a + 24), a == 0, a == 3)
+        mm(B(6), A("I64k"), A("wt"), False, True)
+        useless(t)
+        tt(A("tkb"), B(5, 0, 24), A("z"), ALU.mult)
         tt(A("E2"), IND(A("tkb"), A("rep", 0, 24)), A("FQ"), ALU.mult, xr=[A("rep", 0, 24)])
-        ts(A("E2", rho, C, 16), A("Ee"), 256.0, ALU.add)
+        ts(A("E2", rho, C, 16), A("Dd"), 256.0, ALU.min)
         turn(A("E2T"), A("E2"))
         mm(B(5), A("Ir_%d" % t), A("x%d" % t), True, False)
         mm(B(5), A("I1"), A("E2T"), False, True)
@@ -425,91 +476,103 @@ def rank_program(g, core, T, topo):
     def useless(t):
         if t == RO - 1:
             return
-        run("v", lambda q: q.tensor_reduce(A("zr", 0, 1)[0], A("z")[0], AX.X, ALU.add), [A("z")], [A("zr", 0, 1)])
-        mm(B(7, 0, 1), A("onf"), A("zr", 0, 1), True, True)
-        cp(A("mi", 0, 1), B(7, 0, 1))
-        ts(A("ma", 0, 1), A("mi", 0, 1), 255, ALU.bitwise_and)
-        ts(A("mf", 0, 1), A("ma", 0, 1), 16.0, ALU.mult)
-        ts(A("thr"), A("thb"), A("mf", 0, 1), ALU.add)
+        one1 = A("zr", 0, 1)
+        run("a", lambda q: q.activation(A("zc")[0], A("z")[0], AF.Copy, accum_out=one1[0]), [A("z")], [A("zc"), one1])
+        mm(B(3, 0, 1), A("onf"), one1, True, True)
+        act(A("ma", 0, 1), B(3, 0, 1), AF.Identity, scale=1.0 / 4096, bias=-255.0 / 512)
+        act(A("mb", 0, 1), A("ma", 0, 1), AF.Identity, bias=MAGIC)
+        act(A("mc", 0, 1), A("mb", 0, 1), AF.Identity, scale=-4096.0, bias=4096.0 * MAGIC)
+        act(A("mf", 0, 1), B(3, 0, 1))
 
-    HB = (4, 6)
+    def limits(t):
+        if t < RO - 1:
+            ts(A("thr"), A("thb"), A("mf", 0, 1), ALU.add, A("mc", 0, 1), ALU.add)
 
     def claims1(t):
         turn(A("KM"), B(6))
         top(A("MS"), A("KM"), A("RS"))
         ts(A("xp"), LAST("MS"), (1 << 24) | 4095, ALU.bitwise_and)
         ts(A("xpf"), A("xp"), -2048.0, ALU.add, 32768.0, ALU.min)
-        for h in range(2):
-            c0, c1, rp = 192 * h, 192 * h + 192, A("rep", 12 * h, 12 * h + 12)
-            mm(B(HB[h], c0, c1), A("I1"), A("MO", c0, c1), True, False)
-            tt(A("xd", c0, c1), IND(A("xpf"), rp), A("MD", c0, c1), ALU.mult, xr=[rp])
-            mm(B(HB[h], c0, c1), A("G2f"), A("xd", c0, c1), False, True)
-            act(A("RBs", c0, c1), B(HB[h], c0, c1))
+        rp = A("RP", 0, 24)
+        mm(B(4), A("I1"), A("MO"), True, False)
+        tt(A("xd"), IND(A("xpf"), rp), A("MD"), ALU.mult, xr=[rp])
+        mm(B(4), A("G2f"), A("xd"), False, True)
+        mm(B(6, 0, 192), A("G2f"), A("xd", 0, 192), True, True)
+        act(A("RBs", 0, C), B(4))
+        act(A("RBs", C, C + 192), B(6, 0, 192))
 
     def claims2(t):
-        for h in range(2):
-            c0, c1, rp = 192 * h, 192 * h + 192, A("rep", 12 * h, 12 * h + 12)
+        for rp, c0, c1 in ((A("RP", 0, 24), 0, C), (A("RP", 12, 24), C, C + 192)):
             tt(A("Eq", c0, c1), IND(A("xpf"), rp), A("RBs", c0, c1), ALU.is_equal, xr=[rp])
         top(A("lost"), A("Eq"), A("RSb"))
-        mm(B(7, 0, 24), A("PLf"), A("xpf"), True, False)
-        mm(B(7, 0, 24), A("PL8"), LAST("lost"), False, True)
+        mm(B(4, 0, 24), A("I1"), A("HW", 0, 24), True, False)
+        for b in range(2):
+            mm(B(4, 12 * b, 12 * b + 12), A("PLf"), A("xpf", b, 24, 2), False, False)
+        for n in range(3):
+            for b in range(2):
+                h = min(n, 1)
+                mm(B(4, 12 * b + h, 12 * b + 12, 2), A("PL8"), A("lost", 15 + 16 * (12 * n + b), 192 * n + 192, 32), False, n == 2 and b == 1)
+        limits(t)
+
+    def claims3a(t):
+        for h in range(2):
+            ts(A("oG", h, 24, 2), B(4, h, 24, 2), 2048.0, ALU.add, F(10 + 9 * h), ALU.min)
 
     def claims3(t):
-        for b in range(2):
-            ts(A("oG", 12 * b, 12 * b + 12), B(7, b, 24, 2), 2048.0, ALU.add, F(10), ALU.min)
-        ts(A("oS", 0, 48, 2), B(7, 0, 24), 2048.0, ALU.add, F(10), ALU.min)
         for b in range(2):
             o = A("oG", 12 * b, 12 * b + 12)
             tt(A("V", 192 * b, 192 * b + 192), IND(A("U"), o), A("nB", b, C, 2), ALU.mult, xr=[o])
         for b in (1, 0):
-            for k in range(11, -1, -1):
-                o = A("oS", 2 * (2 * k + b), 2 * (2 * k + b) + 1)
-                cp(IND(A("U"), o), A("V", 192 * b + 16 * k, 192 * b + 16 * k + 16), xr=[o])
+            for k in range(5, -1, -1):
+                o = A("oG", 12 * b + 2 * k, 12 * b + 2 * k + 2)
+                cp(IND(A("U"), o), A("V", 192 * b + 32 * k, 192 * b + 32 * k + 32), xr=[o])
 
+    codes0(0)
     codes1(0)
     constants2()
     constants3()
     codes2(0)
     for t in range(RO):
-        starts(t)
-        gather(0)
+        if t == 0:
+            starts(t)
+            starts1(t)
         ts(A("cf"), A("t3"), 4096, ALU.min, -2048.0, ALU.add)
-        for k in range(1, NCH):
+        for k in range(NCH):
             gather(k)
         starts2(t)
+        starts3(t)
         for k in range(NCH):
             price(k)
             gturn(k)
-            gains(k)
-            for j in VOTES[k]:
-                votes(j)
+            sums(SUMS[k])
             if t == 0 and k == 0:
                 constants4()
             if t == 0 and k == 1:
-                cp(A("thb"), B(7, 0, 24))
-                cp(A("thr"), A("thb"))
-        best1(t)
-        level(t)
-        best2(t)
-        for j in VOTES[NCH]:
-            votes(j)
-        if t == 0:
-            constants5()
+                constants4b()
         highs(t)
-        mm(B(5), A("I1"), A("hib"), False, True)
-        if t < RO - 1:
-            constants6(t + 1)
-        claims1(t)
-        turn(A("FQ"), A("FO"))
-        vote(t)
-        update(t)
-        notb(t)
-        useless(t)
-        claims2(t)
-        if t < RO - 1:
-            codes1(t + 1)
         if t == 1:
             constants7()
+        if t < RO - 1:
+            constants6(t + 1)
+        turn(A("FQ"), A("FO"))
+        for c0, c1 in CHUNKS:
+            mm(B(5, c0, c1), A("hib", c0, c1), A("I1"), False, c1 == C)
+        best1(t)
+        vote(t)
+        best2(t)
+        if t == 0:
+            constants5()
+        update(t)
+        claims1(t)
+        if t < RO - 1:
+            codes0(t + 1)
+        notb(t)
+        claims2(t)
+        claims3a(t)
+        if t < RO - 1:
+            starts(t + 1)
+            codes1(t + 1)
+            starts1(t + 1)
         claims3(t)
         if t < RO - 1:
             codes2(t + 1)

import numpy as np
from concourse.mybir import AluOpType as ALU, AxisListType as AX, ActivationFunctionType as AF

C, W, RO = 384, 4096, 5
VOID = -128.0
UW = W + 48
GTW = 16 * C + 16
MAGIC = 12582912.0
BIG = 1.0e9

SCRATCH = {}
SEMAPHORES = ["sv", "sa", "sp", "sg", "ld0", "ld1", "ld2", "ld3", "ld4", "st0", "st1", "out", "out2"] + ["arr%d" % t for t in range(RO)]
VIEW = {}


def _pack(buf, names, cols, dtype):
    step = -(-cols // 32) * 32
    for k, n in enumerate(names.split()):
        VIEW[n] = (buf, k * step, cols)
    SCRATCH[buf] = ("sbuf", [128, step * len(names.split())], dtype)


def _sb(names, cols, dtype):
    for n in names.split():
        SCRATCH[n] = ("sbuf", [128, cols], dtype)


_sb("U", UW, "bfloat16")
_sb("tsti pi3 t2 t3 KS VS MS", C, "int32")
_sb("prb prp nn hib FO FQ E2 E2T ones MO nBQ nB V wt x0 x1 x2 x3 x4 xo0 xo1", C, "bfloat16")
_sb("Eq lost RSb", C + 192, "bfloat16"), _sb("RBs", C + 192, "float32")
_sb("aS t1 h0 h1 KQ KM MD yo RS", C, "float32"), _sb("cf xd", C, "float16")
_sb("got R", 16 * C, "bfloat16")
_sb("GT", GTW, "bfloat16")
_sb("yco", 256, "float32")
_sb("RY", W // 2, "bfloat16"), _sb("ys", W // 2, "float32")
_sb("cu", C, "uint16")
_sb("rep rep15 wl oG RP", 32, "uint16")
_pack("packI", "K Ai Bi Av xp thi mi L1 L2 L3", 24, "int32")
_pack("packF", "z z8 Cc Dd al lz tkm xpf thr thb thR zr zc ma mb mc mf thf", 24, "float32")
_pack("packB", "val tkb tkr CWh CWl", 24, "bfloat16")
_sb("pc", 32, "int32"), _sb("pf", 32, "float32")
_sb("uA mB sL sG sH", 128, "int32"), _sb("sT0 sT1", 128, "int32"), _sb("iN", 160, "int32")
_sb("uM uD", 128, "float32")
_sb("rK", RO * 128, "int32"), _sb("rKh rKl", RO * 128, "int32"), _sb("rKhb rKlb", RO * 128, "bfloat16")
_sb("r1", 128, "int32"), _sb("rH rM", 128, "bfloat16"), _sb("rV", C, "bfloat16")
_sb("I1 Iv I16 I64k Im256 Blk TriM T00 T01 T10 T11 PL8", 128, "bfloat16")
_pack("packP", " ".join("P2_%d Pn_%d Cm_%d Ir_%d" % (t, t, t, t) for t in range(RO)), 128, "bfloat16")
_sb("BO", 8, "bfloat16"), _sb("HW", 224, "bfloat16"), _sb("X MK", 96, "bfloat16"), _sb("mk", 96, "int32"), _sb("L96", 8, "uint16")
_sb("J0 J1", 160, "float16")
_sb("PLf onf THl", 128, "float32"), _sb("G2f I1h", 128, "float16")
for _k in range(8):
    SCRATCH["B%d" % _k] = ("psum", [128, 512], "float32")
PB = (0, 1, 7)

CHUNKS = [(0, 128), (128, 256), (256, 384)]
GATH = [[("a", 0, 64), ("v", 64, 128)], [("a", 128, 256)], [("a", 256, 384)]]
NCH = len(CHUNKS)
SUMS = [[("v", 0, 128), ("g", 0, 128)], [("v", 128, 256), ("g", 128, 256)], [("g", 256, 384), ("v", 256, 384)], []]


def rank_program(g, core, T, topo):
    rank = T.rank_of(core)
    if rank is None:
        return
    Q = {"v": g.vector, "a": g.scalar, "p": g.tensor, "g": g, "y": g.sync}
    sem = {"v": T.sem.sv, "a": T.sem.sa, "p": T.sem.sp, "g": T.sem.sg}
    cnt, clock, snap, hist = {}, {e: {} for e in Q}, {}, {}

    def A(name, c0=0, c1=None, step=1, p=128):
        name, base, cols = VIEW.get(name, (name, 0, SCRATCH.get(name, (0, (0, 0)))[1][1]))
        c0, c1 = base + c0, base + (cols if c1 is None else c1)
        ap = T[name][0:p, c0:c1:step] if step != 1 else T[name][0:p, c0:c1]
        return (ap, name, c0, c1, step)

    def IND(win, off):
        return (win[0].indirect(off[0]),) + tuple(win[1:])

    def meet(a, b):
        if a[1] >= b[2] or b[1] >= a[2]:
            return False
        if a[3] == b[3] and a[3] > 1 and (a[1] - b[1]) % a[3]:
            return False
        return True

    def need(e, reads, writes):
        want = {}

        def ask(f, n):
            want[f] = max(want.get(f, 0), n)
        for x, wr in [(x, False) for x in reads] + [(x, True) for x in writes]:
            ps = SCRATCH[x[1]][0] == "psum"
            for h in hist.get(x[1], []):
                hit = meet((0,) + tuple(x[2:]), (0,) + h[1:4])
                if h[4] != e:
                    if ps or (hit and (wr or h[6])):
                        ask(h[4], h[5])
                elif hit and (wr or h[6]) and e != "p":
                    ask(h[4], h[5])
        for f in sorted(want, key=lambda k: -want[k]):
            if clock[e].get(f, 0) < want[f]:
                Q[e].wait_ge(sem[f], want[f])
                for k, n in snap[(f, want[f])].items():
                    clock[e][k] = max(clock[e].get(k, 0), n)
                clock[e][f] = max(clock[e].get(f, 0), want[f])

    def note(f, n, e, reads, writes):
        snap[(f, n)] = dict(clock[e])
        for x in writes:
            old = hist.get(x[1], [])
            hist[x[1]] = [h for h in old if not (x[4] == 1 and h[1] >= x[2] and h[2] <= x[3] and (clock[e].get(h[4], 0) >= h[5] or h[4] == f))]
            hist[x[1]].append((0, x[2], x[3], x[4], f, n, True))
        for x in reads:
            L = hist.setdefault(x[1], [])
            L[:] = [h for h in L if not (not h[6] and h[4] == f and h[1:4] == tuple(x[2:5]))]
            L.append((0, x[2], x[3], x[4], f, n, False))

    def run(e, make, reads, writes):
        need(e, reads, writes)
        ins = make(Q[e])
        cnt[e] = cnt.get(e, 0) + 1
        ins.then_inc(sem[e], 1)
        note(e, cnt[e], e, reads, writes)

    def dma(e, out, in_, s, oap=None, iap=None):
        reads, writes = [x for x in (in_,) if x], [x for x in (out,) if x]
        need(e, reads, writes)
        Q[e].dma_start(out[0] if out else oap, in_[0] if in_ else iap).then_inc(T.sem[s], 16)
        sem[s] = T.sem[s]
        cnt[s] = cnt.get(s, 0) + 16
        note(s, cnt[s], e, reads, writes)

    def mm(out, l, r, start, stop):
        run("p", lambda q: q.matmul(out[0], l[0], r[0], start, stop), [l, r], [out])

    def tt(out, a, b, op, xr=()):
        run("v", lambda q: q.tensor_tensor(out[0], a[0], b[0], op), [a, b] + list(xr), [out])

    def ts(out, a, s1, op0, s2=None, op1=None):
        xr = [s for s in (s1, s2) if isinstance(s, tuple)]
        v1 = s1[0] if isinstance(s1, tuple) else s1
        v2 = s2[0] if isinstance(s2, tuple) else s2
        if op1 is None:
            run("v", lambda q: q.tensor_scalar(out[0], a[0], v1, None, op0), [a] + xr, [out])
        else:
            run("v", lambda q: q.tensor_scalar(out[0], a[0], v1, v2, op0, op1), [a] + xr, [out])

    def cp(out, a, xr=()):
        run("v", lambda q: q.tensor_copy(out[0], a[0]), [a] + list(xr), [out])

    def turn(out, a):
        run("v", lambda q: q.transpose(out[0], a[0]), [a], [out])

    def ms(out, c):
        run("v", lambda q: q.memset(out[0], c), [], [out])

    def act(out, a, func=AF.Copy, xr=(), **kw):
        run("a", lambda q: q.activation(out[0], a[0], func, **kw), [a] + list(xr), [out])

    def iota(out, pattern, base, cm):
        run("g", lambda q: q.iota(out[0], pattern, base, cm), [], [out])

    def sel(out, a, pattern, op, fill, base, cm):
        run("g", lambda q: q.affine_select(out[0], a[0], pattern, op, fill, base, cm), [a], [out])

    B = lambda k, c0=0, c1=C, step=1: A("B%d" % k, c0, c1, step)

    def top(out, src, reset):
        run("v", lambda q: q.tensor_tensor_scan(out[0], reset[0], src[0], -BIG, ALU.min, ALU.max), [src, reset], [out])

    LAST = lambda n: A(n, 15, C, 16)

    dma("y", A("tsti"), None, "ld0", iap=T.tst[:])
    dma("a", A("prb"), None, "ld1", iap=T.pr[:])
    dma("a", A("thi", 0, 1, 1, 8), None, "ld2", iap=T.th[:])
    dma("y", A("U", 0, 2048), None, "ld3", iap=T.cov[:, 0:2048])
    dma("a", A("U", 2048, 4096), None, "ld4", iap=T.cov[:, 2048:4096])

    iota(A("pc", 0, 1), [[0, 1]], 0, 1)
    iota(A("uA"), [[-1, 128]], 256, 1)
    iota(A("mB"), [[1, 8], [0, 16]], 0, 0)
    iota(A("rK"), [[77, RO], [0, 8], [613, 16]], 0, 0)
    iota(A("r1"), [[0, 8], [-1, 16]], 15, 0)
    iota(A("iN"), [[1, 160]], -16, 0)
    iota(A("K"), [[1, 24]], 0, 0)
    iota(A("pi3"), [[0, 24], [1, 16]], 0, 0)
    iota(A("sL"), [[32, 4], [1, 2], [2, 16]], 0, 0)
    iota(A("sG"), [[2, 4], [0, 16], [1, 2]], 0, 0)
    iota(A("sH"), [[1, 4], [0, 32]], 0, 0)
    ms(A("ones"), 1.0)
    iota(A("mk"), [[0, 12], [1, 4], [0, 2]], 0, 0)
    P = lambda k: A("pc", k, k + 1)
    F = lambda k: A("pf", k, k + 1)
    ts(P(1), P(0), 4, ALU.arith_shift_right)
    ts(P(3), P(0), 15, ALU.bitwise_and)
    ts(P(2), P(1), 16, ALU.mult)
    cp(A("pf", 0, 4), A("pc", 0, 4))
    ts(A("uA"), A("uA"), 15, ALU.bitwise_and)
    ts(A("uD"), A("mB"), F(1), ALU.subtract, -16.0, ALU.mult)
    tt(A("uM"), A("uA"), A("uD"), ALU.add)
    ts(A("Iv"), A("uM"), 0.0, ALU.is_equal, -360448.0, ALU.mult)

    def perms(t):
        ts(A("P2_%d" % t), A("uM"), t + 1.0, ALU.is_equal, 2.0, ALU.mult)
        act(A("Pn_%d" % t), A("P2_%d" % t), scale=-256.0)
        ts(A("Cm_%d" % t), A("uM"), t + 1.0, ALU.is_equal, -131072.0, ALU.mult)
        tt(A("Cm_%d" % t), A("Cm_%d" % t), A("Iv"), ALU.add)

    def restmats(t):
        ts(F(12 + t), F(3), float(5 * t % 16), ALU.not_equal)
        act(A("Ir_%d" % t), A("I1"), scale=F(12 + t)[0], xr=[F(12 + t)])
    perms(0)
    row = lambda n, c0=0: A(n, c0, c0 + 128, 1, 1)
    one = lambda c0=0, c1=C: A("ones", c0, c1, 1, 1)

    def rows(c0, c1):
        R0 = lambda n: A(n, c0, c1, 1, 1)
        ts(R0("rKh"), R0("rK"), 8, ALU.arith_shift_right, 15, ALU.bitwise_and)
        ts(R0("rKhb"), R0("rKh"), 4096.0, ALU.mult)
        ts(R0("rKl"), R0("rK"), 255, ALU.bitwise_and)
        ts(R0("rKlb"), R0("rKl"), 16.0, ALU.mult)
    rows(0, 128)
    for b in range(2):
        cp(A("x0", b, C, 2), A("tsti", 192 * b, 192 * b + 192))

    def constants2():
        ms(A("U", W, W + 16), VOID)
        ms(A("U", W + 16, UW), 0.0)
        ts(A("I1"), A("uM"), 0.0, ALU.is_equal)
        act(A("I16"), A("I1"), scale=16.0)
        act(A("Im256"), A("I1"), scale=-256.0)
        act(A("I64k"), A("I1"), scale=65536.0)
        for b in range(2):
            act(A("prp", b, C, 2), A("prb", 192 * b, 192 * b + 192))
        for k in range(3):
            for j in range(4):
                mm(B(PB[k], j, 512, 4), A("I1"), A("prp", 128 * k, 128 * k + 128), True, True)
        cp(row("rH"), row("r1"))
        ts(A("rV", 0, C, 1, 1), A("pi3", 0, C, 1, 1), -256.0, ALU.mult, 3840.0, ALU.add)
        ts(row("rM"), row("r1"), 4096.0, ALU.mult, 2048.0, ALU.add)

    def constants3():
        ts(A("BO"), A("iN", 16, 24), F(1), ALU.is_equal, 4096.0, ALU.mult)
        ts(P(11), P(1), 1, ALU.bitwise_and)
        ts(P(8), P(11), 999, ALU.mult)
        ts(P(9), P(11), 999, ALU.mult, -999, ALU.add)
        tt(P(8), P(0), P(8), ALU.subtract)
        tt(P(9), P(0), P(9), ALU.add)
        ts(P(4), P(0), 1, ALU.bitwise_and)
        ts(P(5), P(0), 31, ALU.bitwise_and)
        ts(P(6), P(0), 1, ALU.arith_shift_right)
        ts(P(7), P(0), 5, ALU.arith_shift_right)
        ts(P(17), P(0), 5, ALU.arith_shift_right)
        ts(P(18), P(0), 31, ALU.bitwise_and)
        ts(P(5), P(5), 1, ALU.arith_shift_right)
        ts(P(7), P(7), 2, ALU.mult)
        ts(P(10), P(3), W + 16, ALU.add)
        tt(P(7), P(7), P(4), ALU.add)
        cp(A("pf", 4, 12), A("pc", 4, 12))
        cp(A("thf", 0, 1, 1, 8), A("thi", 0, 1, 1, 8))
        ts(A("mi", 0, 24), A("K", 0, 24), 1, ALU.bitwise_and)
        ts(A("THl", 0, 128, 1, 8), A("sH", 0, 128, 1, 8), A("pf", 6, 7, 1, 8), ALU.is_equal)
        ts(A("thR", 0, 24, 1, 8), A("mi", 0, 24, 1, 8), A("pf", 4, 5, 1, 8), ALU.is_equal, 16.0, ALU.mult)
        ts(A("thR", 0, 24, 1, 8), A("thR", 0, 24, 1, 8), A("thf", 0, 1, 1, 8), ALU.mult)
        mm(B(6, 0, 24), A("THl", 0, 128, 1, 8), A("thR", 0, 24, 1, 8), True, True)
        ts(A("I1h"), A("uM"), 0.0, ALU.is_equal)
        for g2 in range(2):
            ts(A("J%d" % g2), A("iN"), F(8 + g2), ALU.is_equal)
        ts(A("Blk"), A("mB"), F(1), ALU.is_equal)
        sel(A("TriM"), A("Blk"), [[1, 128]], ALU.is_gt, 0.0, 0, -1)
        ms(A("sT0"), -1000), ms(A("sT1"), -1000)
        iota(A("sT0", 0, 128, 2), [[32, 4], [1, 2], [2, 8]], 0, 0)
        iota(A("sT1", 1, 128, 2), [[32, 4], [1, 2], [2, 8]], 0, 0)
        tt(A("TriM"), A("TriM"), A("I1"), ALU.subtract)
        cp(A("thb"), B(6, 0, 24))
        cp(A("thr"), A("thb"))
        ms(A("RS"), BIG)
        sel(A("RS"), A("RS"), [[0, 24], [1, 16]], ALU.not_equal, -BIG, 0, 0)

    def constants4():
        ms(A("GT", 16 * C, GTW), VOID)
        for q3 in range(2):
            for g2 in range(2):
                ts(A("T%d%d" % (q3, g2)), A("sT%d" % g2), 16.0 * q3, ALU.add, F(0), ALU.is_equal)
        ts(A("CWh"), A("K", 0, 24), 256.0, ALU.mult)
        ts(A("CWl"), A("ones", 0, 24), F(3), ALU.mult, 16.0, ALU.mult)
        ts(A("CWl"), A("CWl"), 15.0, ALU.add)
        cp(A("rep", 0, 24), A("K", 0, 24))
        ts(A("rep15", 0, 24), A("K", 0, 24), 16.0, ALU.mult, 15.0, ALU.add)
        restmats(0)

    def constants4b():
        cp(A("pf", 17, 19), A("pc", 17, 19))
        ms(A("HW"), 0.0)
        ts(A("L1", 0, 6), A("K", 0, 6), 16.0, ALU.mult, F(3), ALU.add)
        ts(A("L2", 0, 6), A("L1", 0, 6), 43.0, ALU.mult)
        ts(A("MK"), A("mk"), F(17), ALU.is_equal)
        ts(A("HW", 96, 128), A("iN", 16, 48), F(18), ALU.is_equal)
        ts(A("L2", 0, 6), A("L2", 0, 6), 10, ALU.arith_shift_right)
        ts(A("L3", 0, 6), A("L2", 0, 6), -24.0, ALU.mult)
        tt(A("L1", 0, 6), A("L1", 0, 6), A("L3", 0, 6), ALU.add)
        ts(A("L2", 0, 6), A("L2", 0, 6), 2.0, ALU.mult)
        ts(A("L3", 0, 6), A("L1", 0, 6), 1, ALU.bitwise_and)
        ts(A("L1", 0, 6), A("L1", 0, 6), 24, ALU.bitwise_and)
        tt(A("L2", 0, 6), A("L2", 0, 6), A("L3", 0, 6), ALU.add)
        tt(A("L1", 0, 6), A("L1", 0, 6), A("L2", 0, 6), ALU.add)
        cp(A("L96", 0, 6), A("L1", 0, 6))

    def constants5():
        ts(A("MD"), A("pi3"), F(5), ALU.is_equal)
        ts(A("MO"), A("pi3"), F(5), ALU.is_ge, 32768.0, ALU.mult)
        ts(A("PLf"), A("sL"), F(0), ALU.is_equal)
        act(A("PL8"), A("PLf"), scale=8192.0)
        ts(A("G2f"), A("sG"), F(7), ALU.is_equal)
        act(A("onf"), A("I1"), AF.Identity, scale=0.0, bias=16.0)
        act(A("RSb", 0, C), A("RS"))
        act(A("RSb", C, C + 192), A("RS", 0, 192))
        L1, L2, L3 = A("L1"), A("L2"), A("L3")
        ts(L1, A("K"), 12.0, ALU.is_ge)
        ts(L2, L1, -12.0, ALU.mult)
        tt(L2, L2, A("K"), ALU.add)
        ts(L1, L1, 2.0, ALU.mult)
        ts(L3, L2, 1, ALU.bitwise_and)
        ts(L2, L2, 2.0, ALU.mult)
        tt(L1, L1, L3, ALU.subtract)
        tt(L1, L1, L2, ALU.add)
        cp(A("RP", 0, 24), L1)
        ts(F(19), F(10), 16.0, ALU.add)

    def constants6(t):
        rows(128 * t, 128 * t + 128)
        perms(t)
        restmats(t)

    def constants7():
        act(A("RY"), A("U", 0, W // 2), AF.Identity, scale=0.0, bias=1.0)
        sel(A("RY"), A("RY"), [[0, W // 32], [1, 16]], ALU.not_equal, 0.0, 0, 0)

    def codes0(t):
        mm(B(2), one(0, 128), one(), True, False)
        mm(B(3), row("rKhb", 128 * t), one(), True, False)
        mm(B(3), row("rKlb", 128 * t), one(), False, False)

    def codes1(t):
        x = A("x%d" % t)
        act(A("nn"), x, AF.Relu, bias=-255.0)
        act(A("aS"), x, AF.Identity, bias=1.0, scale=2.0)
        mm(B(2), A("P2_%d" % t), x, False, False)
        mm(B(2), A("Pn_%d" % t), A("nn"), False, True)
        mm(B(3), A("Cm_%d" % t), A("nn"), False, True)

    def codes2(t):
        for c0, c1 in (CHUNKS[0], (CHUNKS[0][1], C)):
            tt(A("t1", c0, c1), A("aS", c0, c1), B(2, c0, c1), ALU.mult)
            tt(A("t2", c0, c1), A("t1", c0, c1), B(3, c0, c1), ALU.add)
            ts(A("t3", c0, c1), A("t2", c0, c1), 4, ALU.arith_shift_right, 0x8FFF, ALU.bitwise_and)
            ts(A("cu", c0, c1), A("t3", c0, c1), 4096, ALU.min)

    def starts(t):
        mm(B(4), row("rH"), one(), True, False)
        mm(B(4), A("Im256"), A("prp"), False, False)

    def starts1(t):
        mm(B(5), one(0, 128), A("rV", 0, C, 1, 1), True, False)

    def starts2(t):
        mm(B(3), A("TriM"), A("nn"), True, False)
        mm(B(3), one(0, 128), one(), False, True)
        mm(B(2), A("I1h"), A("cf"), True, True)

    def starts3(t):
        mm(B(6), row("rM"), one(), True, False)
        for b in range(2):
            for g2 in range(2):
                s = 16 + 16 * (g2 - b)
                mm(B(6, g2, C, 2), A("J%d" % g2, s, s + 128), A("cf", b, C, 2), False, False)

    def highs(t):
        act(A("h0"), B(2), AF.Identity, bias=128.0 - 0.46875, scale=0.0625)
        act(A("h1"), A("h0"), AF.Identity, bias=MAGIC)
        act(A("FO"), B(3), AF.Relu, bias=1.0, scale=-1.0)
        act(A("hib"), A("h1"), AF.Identity, bias=-MAGIC)

    def gather(k):
        for e, c0, c1 in GATH[k]:
            out, win, off = A("got", 16 * c0, 16 * c1), A("U"), A("cu", c0, c1)
            (act if e == "a" else cp)(out, IND(win, off), xr=[off])

    def price(k):
        c0, c1 = CHUNKS[k]
        n, f = 4 * (c1 - c0), 4 * (c0 % 128)
        for s in range(4):
            r = 4 * C * s + 4 * c0
            tt(A("R", r, r + n), A("got", 16 * c0 + s, 16 * c1, 4), B(PB[c0 // 128], f, f + n), ALU.max)

    def gains(c0, c1):
        for i in range(16):
            r = 4 * C * (i % 4) + i // 4
            mm(B(4, c0, c1), A("I16"), A("R", r + 4 * c0, r - i // 4 + 4 * c1, 4), False, c1 == C and i == 15)

    def votes(c0, c1):
        for i in range(16):
            mm(B(5, c0 + i, c1, 16), A("got", 16 * c0 + i, 16 * c1, 16), A("BO"), False, False)

    def sums(L):
        for what, c0, c1 in L:
            (gains if what == "g" else votes)(c0, c1)

    def gturn(k):
        c0, c1 = CHUNKS[k]
        turn(A("GT", 16 * c0, 16 * c1), A("got", 16 * c0, 16 * c1))

    def best1(t):
        turn(A("KQ"), B(4))
        top(A("KS"), A("KQ"), A("RS"))
        ts(A("Ai"), LAST("KS"), 15, ALU.bitwise_and)
        tt(A("z"), LAST("KS"), A("thr"), ALU.is_lt)
        ts(A("z8"), A("z"), 8192.0, ALU.mult)
        tt(A("val"), A("z8"), A("Ai"), ALU.subtract)
        mm(B(4, 0, 24), A("I1"), A("CWh"), True, False)
        mm(B(4, 0, 24), A("I1"), A("CWl"), False, False)
        for q3 in range(2):
            for g2 in range(2):
                mm(B(4, q3, 24, 2), A("T%d%d" % (q3, g2)), A("val", g2, 24, 2), False, q3 == 1 and g2 == 1)

    def best2(t):
        ts(A("wl", 0, 24), B(4, 0, 24), 16.0 * C, ALU.min)
        act(A("wt"), IND(A("GT"), A("wl", 0, 24)), xr=[A("wl", 0, 24)])

    def notb(t):
        tt(A("nBQ"), IND(A("KS"), A("rep15", 0, 24)), A("KQ"), ALU.not_equal, xr=[A("rep15", 0, 24)])
        turn(A("nB"), A("nBQ"))

    def level(t):
        ts(A("Bi"), LAST("KS"), 4, ALU.arith_shift_right, 15, ALU.bitwise_and)
        ts(A("Cc"), A("val"), 16.0, ALU.mult, 240.0, ALU.add)
        tt(A("Dd"), A("Bi"), A("Cc"), ALU.add)

    def vote(t):
        top(A("VS"), B(5), A("RS"))

    def update(t):
        rho, xo = (5 * t) % 16, "xo%d" % (t % 2)
        ts(A("Av"), LAST("VS"), 255, ALU.bitwise_and)
        ts(A("al"), LAST("VS"), 0.0, ALU.is_ge)
        ts(A("tkm"), A("Av"), -256.0, ALU.add)
        tt(A("tkr"), A("tkm"), A("al"), ALU.mult)
        tt(A("X"), IND(A("tkr"), A("L96", 0, 6)), A("MK"), ALU.mult, xr=[A("L96", 0, 6)])
        level(t)
        for a in range(4):
            mm(B(5, 0, 24), A("HW", 96 - 32 * a, 224 - 32 * a), A("X", 24 * a, 24 * a + 24), a == 0, a == 3)
        mm(B(6), A("I64k"), A("wt"), False, True)
        useless(t)
        tt(A("tkb"), B(5, 0, 24), A("z"), ALU.mult)
        tt(A("E2"), IND(A("tkb"), A("rep", 0, 24)), A("FQ"), ALU.mult, xr=[A("rep", 0, 24)])
        ts(A("E2", rho, C, 16), A("Dd"), 256.0, ALU.min)
        turn(A("E2T"), A("E2"))
        mm(B(5), A("Ir_%d" % t), A("x%d" % t), True, False)
        mm(B(5), A("I1"), A("E2T"), False, True)
        act(A(xo), B(5))
        if t < RO - 1:
            to = T.cores[(rank + 1) % len(T.cores)]
            rid, pid = topo.addr(to, core)
            eng = topo.engines(core, to)[:8]
            need("g", [A(xo)], [])
            s, a = "st%d" % (t % 2), "arr%d" % (t + 1)
            g.remote_dma(T["x%d" % (t + 1)][:, :], A(xo)[0], T.sem[a], T.sem[s], pid, rid, sum(1 << k for k in eng))
            sem[s] = T.sem[s]
            cnt[s] = cnt.get(s, 0) + len(eng)
            note(s, cnt[s], "g", [A(xo)], [])
            src = T.cores[(rank - 1) % len(T.cores)]
            sem[a], cnt[a] = T.sem[a], len(topo.engines(src, core)[:8])
            snap[(a, cnt[a])] = {}
            hist["x%d" % (t + 1)] = [(0, 0, C, 1, a, cnt[a], True)]

    def useless(t):
        if t == RO - 1:
            return
        one1 = A("zr", 0, 1)
        run("a", lambda q: q.activation(A("zc")[0], A("z")[0], AF.Copy, accum_out=one1[0]), [A("z")], [A("zc"), one1])
        mm(B(3, 0, 1), A("onf"), one1, True, True)
        act(A("ma", 0, 1), B(3, 0, 1), AF.Identity, scale=1.0 / 4096, bias=-255.0 / 512)
        act(A("mb", 0, 1), A("ma", 0, 1), AF.Identity, bias=MAGIC)
        act(A("mc", 0, 1), A("mb", 0, 1), AF.Identity, scale=-4096.0, bias=4096.0 * MAGIC)
        act(A("mf", 0, 1), B(3, 0, 1))

    def limits(t):
        if t < RO - 1:
            ts(A("thr"), A("thb"), A("mf", 0, 1), ALU.add, A("mc", 0, 1), ALU.add)

    def claims1(t):
        turn(A("KM"), B(6))
        top(A("MS"), A("KM"), A("RS"))
        ts(A("xp"), LAST("MS"), (1 << 24) | 4095, ALU.bitwise_and)
        ts(A("xpf"), A("xp"), -2048.0, ALU.add, 32768.0, ALU.min)
        rp = A("RP", 0, 24)
        mm(B(4), A("I1"), A("MO"), True, False)
        tt(A("xd"), IND(A("xpf"), rp), A("MD"), ALU.mult, xr=[rp])
        mm(B(4), A("G2f"), A("xd"), False, True)
        mm(B(6, 0, 192), A("G2f"), A("xd", 0, 192), True, True)
        act(A("RBs", 0, C), B(4))
        act(A("RBs", C, C + 192), B(6, 0, 192))

    def claims2(t):
        for rp, c0, c1 in ((A("RP", 0, 24), 0, C), (A("RP", 12, 24), C, C + 192)):
            tt(A("Eq", c0, c1), IND(A("xpf"), rp), A("RBs", c0, c1), ALU.is_equal, xr=[rp])
        top(A("lost"), A("Eq"), A("RSb"))
        mm(B(4, 0, 24), A("I1"), A("HW", 0, 24), True, False)
        for b in range(2):
            mm(B(4, 12 * b, 12 * b + 12), A("PLf"), A("xpf", b, 24, 2), False, False)
        for n in range(3):
            for b in range(2):
                h = min(n, 1)
                mm(B(4, 12 * b + h, 12 * b + 12, 2), A("PL8"), A("lost", 15 + 16 * (12 * n + b), 192 * n + 192, 32), False, n == 2 and b == 1)
        limits(t)

    def claims3a(t):
        for h in range(2):
            ts(A("oG", h, 24, 2), B(4, h, 24, 2), 2048.0, ALU.add, F(10 + 9 * h), ALU.min)

    def claims3(t):
        for b in range(2):
            o = A("oG", 12 * b, 12 * b + 12)
            tt(A("V", 192 * b, 192 * b + 192), IND(A("U"), o), A("nB", b, C, 2), ALU.mult, xr=[o])
        for b in (1, 0):
            for k in range(5, -1, -1):
                o = A("oG", 12 * b + 2 * k, 12 * b + 2 * k + 2)
                cp(IND(A("U"), o), A("V", 192 * b + 32 * k, 192 * b + 32 * k + 32), xr=[o])

    codes0(0)
    codes1(0)
    constants2()
    constants3()
    codes2(0)
    for t in range(RO):
        if t == 0:
            starts(t)
            starts1(t)
        ts(A("cf"), A("t3"), 4096, ALU.min, -2048.0, ALU.add)
        for k in range(NCH):
            gather(k)
        starts2(t)
        starts3(t)
        for k in range(NCH):
            price(k)
            gturn(k)
            sums(SUMS[k])
            if t == 0 and k == 0:
                constants4()
            if t == 0 and k == 1:
                constants4b()
        highs(t)
        if t == 1:
            constants7()
        if t < RO - 1:
            constants6(t + 1)
        turn(A("FQ"), A("FO"))
        for c0, c1 in CHUNKS:
            mm(B(5, c0, c1), A("hib", c0, c1), A("I1"), False, c1 == C)
        best1(t)
        vote(t)
        best2(t)
        if t == 0:
            constants5()
        update(t)
        claims1(t)
        if t < RO - 1:
            codes0(t + 1)
        notb(t)
        claims2(t)
        claims3a(t)
        if t < RO - 1:
            starts(t + 1)
            codes1(t + 1)
            starts1(t + 1)
        claims3(t)
        if t < RO - 1:
            codes2(t + 1)

    top2 = [A("ys"), A("RY"), A("U", 0, W // 2)]
    run("v", lambda q: q.tensor_tensor_scan(top2[0][0], top2[1][0], top2[2][0], 0.0, ALU.mult, ALU.add), top2[1:], top2[:1])
    for k in range(16):
        mm(B(4, 0, 128), A("I1"), A("U", W // 2 + k, W, 16), k == 0, k == 15)
    for b in range(2):
        act(A("yo", 192 * b, 192 * b + 192), A("xo0", b, C, 2))
    dma("a", None, A("yo"), "out", oap=T.yt[:])
    act(A("yco", 128, 256), B(4, 0, 128))
    cp(A("yco", 0, 128), A("ys", 15, W // 2, 16))
    dma("y", None, A("yco"), "out2", oap=T.yc[:])
    for s in sem:
        if cnt.get(s, 0):
            g.wait_ge(sem[s], cnt[s])
